import numpy as np
import ml_dtypes


def mxq(x, axis, fmt="e4m3"):
    dtype, down = {"e4m3": (ml_dtypes.float8_e4m3fn, 7), "e5m2": (ml_dtypes.float8_e5m2, 14)}[fmt]
    v = np.moveaxis(np.asarray(x, np.float32).astype(ml_dtypes.bfloat16).astype(np.float64), axis, -1)
    blocks = v.reshape(v.shape[:-1] + (-1, 32))
    amax = np.abs(blocks).max(-1, keepdims=True)
    byte = np.maximum(np.where(amax > 0, np.frexp(amax)[1] - 1 + 127, 0) - down, 1)
    scale = np.exp2(byte - 127.0)
    codes = (blocks / scale).astype(np.float32).astype(dtype).astype(np.float64)
    return np.moveaxis((codes * scale).reshape(v.shape), -1, axis)


WIDE = False


def mx_kscale(k):
    if not WIDE:
        return np.ones(k)
    levels = np.array([10, -10, 5, -5, 0])
    if k % 512:
        return np.exp2(np.random.permutation(np.resize(levels, k // 32))).repeat(32)
    a = np.empty((k // 512, 16))
    for p in range(k // 512):
        a[p, :8] = np.random.permutation(np.resize(levels, 8))
        for g in range(8):
            far = levels[np.abs(levels - a[p, g]) >= 10]
            a[p, g + 8] = far[np.random.randint(len(far))]
    return np.exp2(a.ravel()).repeat(32)


def f64(x):
    return np.asarray(x).astype(np.float64)


def striped(idx):
    return np.tile(idx.reshape(-1, 16).T, (8, 1)).astype(np.uint16)


def unstriped(offs):
    return offs[:16].T.reshape(-1).astype(np.int64)


def striped8(idx):
    return np.concatenate([x.reshape(-1, 16).T for x in idx]).astype(np.uint16)


def runs(offs, k):
    lists = np.stack([offs[16 * r : 16 * r + 16].T.reshape(-1) for r in range(8)]).astype(np.int64)
    return lists[np.arange(k) % 512 // 64]


def pack_weight(w):
    k, n = w.shape
    w = f64(np.asarray(w, np.float32).astype(ml_dtypes.bfloat16)).reshape(k // 32, 32, n)
    amax = np.abs(w).max(1)
    byte = np.clip(np.where(amax > 0, np.frexp(amax)[1] - 1 + 127 - 7, 1), 1, 254)
    scaled = (w * np.exp2(127.0 - byte)[:, None, :]).reshape(k, n).astype(np.float32)
    words = np.ascontiguousarray(scaled.reshape(k // 512, 128, 4, n).transpose(0, 1, 3, 2)).astype(ml_dtypes.float8_e4m3fn).view(np.uint8)
    return words, np.ascontiguousarray(byte.astype(np.uint8).reshape(k // 512, 16, n))


def unpack_weight(words, scales):
    g, p, n, _ = words.shape
    vals = np.ascontiguousarray(words).view(ml_dtypes.float8_e4m3fn).astype(np.float64) * np.repeat(np.exp2(scales.astype(np.float64) - 127.0), 8, axis=1)[..., None]
    return vals.transpose(0, 1, 3, 2).reshape(g * 512, n)


E2M1 = np.array([0.0, 0.5, 1.0, 1.5, 2.0, 3.0, 4.0, 6.0, -0.0, -0.5, -1.0, -1.5, -2.0, -3.0, -4.0, -6.0])


def pack_fp4(w):
    k, n = w.shape
    w = f64(np.asarray(w, np.float32).astype(ml_dtypes.bfloat16)).reshape(k // 32, 32, n)
    amax = np.abs(w).max(1)
    mant, ex = np.frexp(amax / 6.0)
    byte = np.clip(np.where(amax > 0, np.where(mant > 0.5, ex, ex - 1) + 127, 1), 1, 254)
    scaled = (w * np.exp2(127.0 - byte)[:, None, :]).reshape(k, n).astype(np.float32)
    c = np.ascontiguousarray(scaled.reshape(k // 512, 128, 4, n).transpose(0, 1, 3, 2)).astype(ml_dtypes.float4_e2m1fn).view(np.uint8) & 0xF
    words = (c[..., 0::2] | (c[..., 1::2] << 4)).reshape(k // 512, 128, 2 * n)
    return np.ascontiguousarray(words), np.ascontiguousarray(byte.astype(np.uint8).reshape(k // 512, 16, n))


def unpack_fp4(words, scales):
    g, _, n = scales.shape
    words = np.ascontiguousarray(words).reshape(g, 128, n, 2)
    nib = np.empty((g, 128, n, 4), np.uint8)
    nib[..., 0::2] = words & 0xF
    nib[..., 1::2] = words >> 4
    vals = E2M1[nib] * np.repeat(np.exp2(scales.astype(np.float64) - 127.0), 8, axis=1)[..., None]
    return vals.transpose(0, 1, 3, 2).reshape(g * 512, n)


def sigmoid(v):
    return 1.0 / (1.0 + np.exp(-np.maximum(v, -700.0)))

def planes(y):
    n, m = y.shape
    v = y.astype(np.float32).astype(ml_dtypes.bfloat16).astype(np.float64).reshape(n // 32, 32, m)
    top = np.abs(v).max(1)
    byte = np.clip(np.where(top > 0, np.frexp(top)[1] - 1 + 127 - 7, 1), 1, 254)
    codes = (v * np.exp2(127.0 - byte)[:, None, :]).reshape(n, m).astype(np.float32).astype(ml_dtypes.float8_e4m3fn).view(np.uint8)
    words = codes.reshape(n // 512, 128, 4, m).transpose(0, 1, 3, 2)
    return np.ascontiguousarray(words), np.ascontiguousarray(byte.astype(np.uint8).reshape(n // 512, 16, m))


K, T, S, N, H = 512, 2048, 512, 512, 512


def setup_inputs():
    n = np.random.standard_normal
    s = mx_kscale(K)[:, None]
    u = mx_kscale(H)
    packed_xT = pack_weight(n((K, T)) * s)
    packed_w1 = pack_fp4(n((K, H)) / np.sqrt(K) / s)
    packed_w2 = pack_fp4(n((K, H)) / np.sqrt(K) / s)
    packed_w3 = pack_fp4(n((K, H)) / np.sqrt(K) / s)
    packed_w4 = pack_fp4(n((H, N)) / np.sqrt(H) / u[:, None])
    return {
        "x_words": packed_xT[0],
        "x_scales": packed_xT[1],
        "w1_words": packed_w1[0],
        "w1_scales": packed_w1[1],
        "w2_words": packed_w2[0],
        "w2_scales": packed_w2[1],
        "w3_words": packed_w3[0],
        "w3_scales": packed_w3[1],
        "gn": (np.random.uniform(0.5, 1.5, (H, 1)) * u[:, None]).astype(np.float32),
        "w4_words": packed_w4[0],
        "w4_scales": packed_w4[1],
        "offs": striped(np.random.permutation(T)[:S]),
        "two": striped(np.random.permutation(T)[:S]),
        "three": striped(np.random.permutation(T)[:S]),
        "n1": striped8(np.stack([np.random.permutation(S) for _ in range(8)])),
        "n2": striped8(np.stack([np.random.permutation(S) for _ in range(8)])),
        "n3": striped8(np.stack([np.random.permutation(S) for _ in range(8)])),
        "n4": striped8(np.stack([np.random.permutation(S) for _ in range(8)])),
        "n5": striped8(np.stack([np.random.permutation(S) for _ in range(8)])),
        "n6": striped8(np.stack([np.random.permutation(S) for _ in range(8)])),
        "n7": striped8(np.stack([np.random.permutation(S) for _ in range(8)])),
    }


def reference(x_words, x_scales, w1_words, w1_scales, w2_words, w2_scales, w3_words, w3_scales, gn, w4_words, w4_scales, offs, two, three, n1, n2, n3, n4, n5, n6, n7):
    x_three = unpack_weight(x_words, x_scales)[:, unstriped(three)]
    b = unpack_fp4(w3_words, w3_scales).T @ x_three
    xq = unpack_weight(x_words, x_scales)[:, unstriped(offs)]
    y = unpack_fp4(w1_words, w1_scales).T @ xq
    x_two = unpack_weight(x_words, x_scales)[:, unstriped(two)]
    d = unpack_fp4(w2_words, w2_scales).T @ x_two
    m1 = y * (sigmoid(d[np.arange(H)[:, None], runs(n2, H)])) - (0.5 * (y[np.arange(H)[:, None], runs(n1, H)]))
    z = f64(gn) * (b * (m1[np.arange(H)[:, None], runs(n3, H)] - m1) + 0.5 * ((b[np.arange(H)[:, None], runs(n5, H)]) * (m1[np.arange(H)[:, None], runs(n4, H)] - m1)))
    h = unpack_fp4(w4_words, w4_scales).T @ mxq(z, 0, "e4m3")
    pa = h[np.arange(N)[:, None], runs(n6, N)]
    pb = h[np.arange(N)[:, None], runs(n7, N)]
    out_0 = np.maximum(np.minimum(h, pa), np.minimum(np.maximum(h, pa), pb))
    return (out_0,) + planes(out_0)

@@ -1,0 +1,289 @@
+from contextlib import ExitStack
+
+import concourse.mybir as mybir
+
+F32 = mybir.dt.float32
+BF16 = mybir.dt.bfloat16
+I32 = mybir.dt.int32
+U32 = mybir.dt.uint32
+U16 = mybir.dt.uint16
+U8 = mybir.dt.uint8
+FP8X4 = mybir.dt.float8_e4m3fn_x4
+FP4X4 = mybir.dt.float4_e2m1fn_x4
+ALU = mybir.AluOpType
+ACT = mybir.ActivationFunctionType
+
+P = 128
+R = 4
+T = 2048
+S = 512
+HALF = 256
+FLOPS = 4 * 2 * 512 * 512 * 512
+OUT_CHUNKS = ((0, 256), (256, 128), (384, 128))
+
+
+def tile_picked_triogatebflowbmed_none_po_kernel(
+    tc, x_words, x_scales, w1_words, w1_scales, w2_words, w2_scales, w3_words, w3_scales, gn,
+    w4_words, w4_scales, offs, two, three, n1, n2, n3, n4, n5, n6, n7, out_0, out_1, out_2,
+):
+    nc = tc.nc
+    with ExitStack() as ctx:
+        sb = ctx.enter_context(tc.tile_pool(name="sb", bufs=1))
+        ps = ctx.enter_context(tc.psum_pool(name="ps", bufs=8))
+
+        def new(name, shape, dtype):
+            return sb.tile(shape, dtype, name=name, align_bytes=64)
+
+        lists = {}
+
+        def load_list(name, src):
+            lists[name] = new("list_" + name, [P, S // 16], U16)
+            nc.sync.dma_start(lists[name][:], src)
+
+        def entries(name, c0, n):
+            return lists[name][:, c0 // 16 : (c0 + n) // 16]
+
+        def load_scale_rows(plane, src):
+            for q in range(4):
+                nc.sync.dma_start(plane[32 * q : 32 * q + 4, :].bitcast(I32), src[0, 4 * q : 4 * q + 4, :].bitcast(I32))
+
+        xs = new("xs", [P, T], U8)
+        nc.vector.memset(xs[:].bitcast(I32), 0)
+        ws_raw = {}
+        for w in (2, 1, 3, 4):
+            ws_raw[w] = new("ws_raw%d" % w, [P, S], U8)
+            nc.vector.memset(ws_raw[w][:].bitcast(I32), 0)
+
+        warm_in = new("warm_in", [P, 1], F32)
+        warm_out = new("warm_out", [P, 1], F32)
+        nc.vector.memset(warm_in[:], 0.0)
+        nc.scalar.activation(warm_out[:], warm_in[:], ACT.Sigmoid)
+
+        w_words = {1: w1_words, 2: w2_words, 3: w3_words, 4: w4_words}
+        w_scales = {1: w1_scales, 2: w2_scales, 3: w3_scales, 4: w4_scales}
+        ww_raw = {}
+        for w in (2, 1, 3, 4):
+            ww_raw[w] = new("ww_raw%d" % w, [P, 2 * S], U8)
+            nc.sync.dma_start(ww_raw[w][:].bitcast(I32), w_words[w][0].bitcast(I32))
+        xw = new("xw", [P, T], I32)
+        nc.sync.dma_start(xw[:], x_words[0].rearrange("p n t -> p (n t)").bitcast(I32))
+        load_list("two", two)
+        load_list("offs", offs)
+        load_list("three", three)
+        load_scale_rows(xs, x_scales)
+        load_scale_rows(ws_raw[2], w_scales[2])
+        load_scale_rows(ws_raw[1], w_scales[1])
+        load_list("n2", n2)
+        load_list("n1", n1)
+        load_scale_rows(ws_raw[3], w_scales[3])
+        gain = new("gain", [P, R], F32)
+        nc.sync.dma_start(gain[:], gn.rearrange("(p t) o -> p (t o)", t=R))
+        load_list("n4", n4)
+        load_list("n3", n3)
+        load_list("n5", n5)
+        load_scale_rows(ws_raw[4], w_scales[4])
+        load_list("n6", n6)
+        load_list("n7", n7)
+
+        ww = {}
+        ws = {}
+
+        def deal_words(w):
+            ww[w] = new("ww%d" % w, [P, 2 * S], U8)
+            nc.vector.tensor_copy(
+                ww[w][:].rearrange("p (t m b) -> p t m b", t=R, b=2),
+                ww_raw[w][:].rearrange("p (m t b) -> p t m b", t=R, b=2),
+            )
+
+        def deal_scales(w):
+            ws[w] = new("ws%d" % w, [P, S], U8)
+            nc.vector.tensor_copy(
+                ws[w][:].rearrange("p (t m) -> p t m", t=R),
+                ws_raw[w][:].rearrange("p (m t) -> p t m", t=R),
+            )
+
+        def product(acc, w, t, codes, scales):
+            nc.tensor.matmul_mx(
+                out=acc,
+                lhsT=ww[w][:, 2 * P * t : 2 * P * (t + 1)].bitcast(FP4X4),
+                lhsT_scale=ws[w][:, P * t : P * (t + 1)],
+                rhs=codes.bitcast(FP8X4),
+                rhs_scale=scales,
+                start=True,
+                stop=True,
+            )
+
+        def pick(name):
+            codes = new("codes_" + name, [P, S], U32)
+            scales = new("scales_" + name, [P, S], U8)
+            nc.vector.tensor_copy(codes[:], xw[:].bitcast(U32).indirect(lists[name][:]))
+            nc.vector.tensor_copy(scales[:], xs[:].indirect(lists[name][:]))
+            return codes, scales
+
+        def project(w, picked):
+            banks = []
+            for t in range(R):
+                bank = ps.tile([P, S], F32, name="bank")
+                product(bank[:], w, t, picked[0][:], picked[1][:])
+                banks.append(bank)
+            return banks
+
+        for w in (2, 1, 3, 4):
+            deal_words(w)
+        x_two = pick("two")
+        deal_scales(2)
+        d_ps = project(2, x_two)
+        x_offs = pick("offs")
+        deal_scales(1)
+        y_ps = project(1, x_offs)
+        x_three = pick("three")
+        deal_scales(3)
+
+        def rows(name):
+            return [new("%s%d" % (name, t), [P, S], F32) for t in range(R)]
+
+        d, gate, yh, yg, m1, m1c, bg = (rows(n) for n in ("d", "gate", "yh", "yg", "m1", "m1c", "bg"))
+        u, v, p, w5 = (rows(n) for n in ("u", "v", "p", "w5"))
+        halves = [slice(0, HALF), slice(HALF, S)]
+        z = [new("z%d" % h, [P, R, HALF], F32) for h in range(2)]
+
+        def leave_banks(t):
+            nc.scalar.copy(d[t][:], d_ps[t][:])
+            for h in range(2):
+                nc.scalar.activation(gate[t][:, halves[h]], d[t][:].indirect(entries("n2", HALF * h, HALF)), ACT.Sigmoid)
+            nc.scalar.activation(yh[t][:], y_ps[t][:], ACT.Copy, scale=-0.5)
+
+        def make_bg(t):
+            bank = ps.tile([P, S], F32, name="bank")
+            product(bank[:], 3, t, x_three[0][:], x_three[1][:])
+            nc.scalar.activation(bg[t][:], bank[:], ACT.Copy, scale=gain[:, t : t + 1])
+
+        def make_yg(t):
+            nc.vector.scalar_tensor_tensor(yg[t][:], yh[t][:], -2.0, gate[t][:], ALU.mult, ALU.mult)
+
+        def fused(dst, window, name, h, other, op):
+            nc.vector.tensor_tensor(dst[:, halves[h]], window[:].indirect(entries(name, HALF * h, HALF)), other[:, halves[h]], op)
+
+        def make_m1(t):
+            for h in range(2):
+                fused(m1[t], yh[t], "n1", h, yg[t], ALU.add)
+            nc.scalar.copy(m1c[t][:], m1[t][:])
+
+        def make_z(t, h):
+            nc.vector.scalar_tensor_tensor(z[h][:, t, :], w5[t][:, halves[h]], 0.5, p[t][:, halves[h]], ALU.mult, ALU.add)
+
+        def weave(engine_copy, dst, src):
+            engine_copy(dst[:].rearrange("p (c i) t -> p c t i", i=4), src[:].rearrange("p t (c i) -> p c t i", i=4))
+
+        leave_banks(0)
+        leave_banks(1)
+        make_yg(0)
+        deal_scales(4)
+        make_m1(0)
+        make_bg(0)
+        for t in range(R - 1):
+            make_bg(t + 1)
+            if t + 2 < R:
+                leave_banks(t + 2)
+            make_yg(t + 1)
+            fused(v[t], m1[t], "n4", 0, m1c[t], ALU.subtract)
+            fused(v[t], m1[t], "n4", 1, m1c[t], ALU.subtract)
+            make_m1(t + 1)
+            fused(u[t], m1[t], "n3", 0, m1c[t], ALU.subtract)
+            fused(u[t], m1[t], "n3", 1, m1c[t], ALU.subtract)
+            fused(w5[t], bg[t], "n5", 0, v[t], ALU.mult)
+            nc.vector.tensor_tensor(p[t][:], u[t][:], bg[t][:], ALU.mult)
+            fused(w5[t], bg[t], "n5", 1, v[t], ALU.mult)
+            make_z(t, 0)
+            make_z(t, 1)
+
+        zb = [new("zb%d" % h, [P, HALF, R], BF16) for h in range(2)]
+        zq = [new("zq%d" % h, [P, HALF], U32) for h in range(2)]
+        zs = [new("zs%d" % h, [P, HALF], U8) for h in range(2)]
+        hw = rows("hw")
+        hc = [new("hc%d" % c, [P, R, n], F32) for c, (c0, n) in enumerate(OUT_CHUNKS)]
+
+        def last_layer(h):
+            nc.vector.quantize_mx(out=zq[h][:].bitcast(FP8X4), scales=zs[h][:], in_=zb[h][:].rearrange("p c t -> p (c t)"))
+            banks = [ps.tile([P, 2, HALF], F32, name="bank") for pair in range(2)]
+            for t in range(R):
+                product(banks[t // 2][:, t % 2, :], 4, t, zq[h][:], zs[h][:])
+            for t in range(R):
+                nc.scalar.copy(hw[t][:, halves[h]], banks[t // 2][:, t % 2, :])
+            for c, (c0, n) in enumerate(OUT_CHUNKS):
+                if c0 // HALF == h:
+                    for pair in range(2):
+                        nc.scalar.copy(hc[c][:, 2 * pair : 2 * pair + 2, :], banks[pair][:, :, c0 - HALF * h : c0 - HALF * h + n])
+
+        t = R - 1
+        fused(v[t], m1[t], "n4", 0, m1c[t], ALU.subtract)
+        fused(u[t], m1[t], "n3", 0, m1c[t], ALU.subtract)
+        fused(w5[t], bg[t], "n5", 0, v[t], ALU.mult)
+        nc.vector.tensor_tensor(p[t][:, halves[0]], u[t][:, halves[0]], bg[t][:, halves[0]], ALU.mult)
+        fused(v[t], m1[t], "n4", 1, m1c[t], ALU.subtract)
+        make_z(t, 0)
+        weave(nc.scalar.copy, zb[0], z[0])
+        fused(u[t], m1[t], "n3", 1, m1c[t], ALU.subtract)
+        fused(w5[t], bg[t], "n5", 1, v[t], ALU.mult)
+        nc.vector.tensor_tensor(p[t][:, halves[1]], u[t][:, halves[1]], bg[t][:, halves[1]], ALU.mult)
+        last_layer(0)
+        make_z(t, 1)
+        weave(nc.vector.tensor_copy, zb[1], z[1])
+        last_layer(1)
+
+        oq = new("oq", [P, S], U32)
+        osc = new("osc", [P, S], U8)
+        out_rows = out_0.rearrange("(p t) s -> p t s", t=R)
+        out_words = out_1[0].rearrange("p n t -> p (n t)").bitcast(I32)
+        da, db, lo, med, res = (
+            [new("%s%d" % (name, c), [P, R, n], F32) for c, (c0, n) in enumerate(OUT_CHUNKS)]
+            for name in ("da", "db", "lo", "med", "res")
+        )
+        resb = [new("resb%d" % c, [P, n, R], BF16) for c, (c0, n) in enumerate(OUT_CHUNKS)]
+
+        def fetch(c, t):
+            c0, n = OUT_CHUNKS[c]
+            nc.vector.tensor_tensor(da[c][:, t, :], hw[t][:].indirect(entries("n6", c0, n)), hc[c][:, t, :], ALU.subtract)
+            nc.vector.tensor_tensor(db[c][:, t, :], hw[t][:].indirect(entries("n7", c0, n)), hc[c][:, t, :], ALU.subtract)
+
+        def flat(tile, ts):
+            return tile[:, ts, :].rearrange("p t n -> p (t n)")
+
+        def step(c, k, ts):
+            if k == 0:
+                nc.vector.scalar_tensor_tensor(flat(lo[c], ts), flat(da[c], ts), 0.0, flat(db[c], ts), ALU.max, ALU.min)
+            elif k == 1:
+                nc.vector.scalar_tensor_tensor(flat(med[c], ts), flat(da[c], ts), 0.0, flat(lo[c], ts), ALU.min, ALU.max)
+            else:
+                nc.vector.tensor_tensor(flat(res[c], ts), flat(med[c], ts), flat(hc[c], ts), ALU.add)
+
+        def hand_out(c, engine_copy):
+            c0, n = OUT_CHUNKS[c]
+            nc.sync.dma_start(out_rows[:, :, c0 : c0 + n], res[c][:])
+            weave(engine_copy, resb[c], res[c])
+
+        def planes(c):
+            c0, n = OUT_CHUNKS[c]
+            nc.vector.quantize_mx(out=oq[:, c0 : c0 + n].bitcast(FP8X4), scales=osc[:, c0 : c0 + n], in_=resb[c][:].rearrange("p c t -> p (c t)"))
+            nc.sync.dma_start(out_words[:, c0 : c0 + n], oq[:, c0 : c0 + n].bitcast(I32))
+
+        every = slice(0, R)
+        last = len(OUT_CHUNKS) - 1
+        for c in range(last + 1):
+            for t in range(R):
+                fetch(c, t)
+                if c > 0 and t < 3:
+                    step(c - 1, t, every)
+            if c > 0:
+                hand_out(c - 1, nc.scalar.copy)
+            if c > 1:
+                planes(c - 2)
+        for k in range(3):
+            step(last, k, slice(0, 2))
+            step(last, k, slice(2, 4))
+        planes(last - 1)
+        hand_out(last, nc.vector.tensor_copy)
+        planes(last)
+        for q in range(4):
+            queue = nc.scalar if q % 2 else nc.sync
+            queue.dma_start(out_2[0, 4 * q : 4 * q + 4, :].bitcast(I32), osc[32 * q : 32 * q + 4, :].bitcast(I32))

@@ -1,6 +1,7 @@
 from contextlib import ExitStack
 
 import concourse.mybir as mybir
+from concourse.masks import make_identity
 
 F32 = mybir.dt.float32
 BF16 = mybir.dt.bfloat16
@@ -29,10 +30,13 @@ def tile_picked_triogatebflowbmed_none_po_kernel(
     nc = tc.nc
     with ExitStack() as ctx:
         sb = ctx.enter_context(tc.tile_pool(name="sb", bufs=1))
-        ps = ctx.enter_context(tc.psum_pool(name="ps", bufs=8))
+        ps = ctx.enter_context(tc.psum_pool(name="ps", bufs=1))
 
-        def new(name, shape, dtype):
-            return sb.tile(shape, dtype, name=name, align_bytes=64)
+        def new(name, shape, dtype, tag=""):
+            return sb.tile(shape, dtype, name=name, tag=tag, align_bytes=64)
+
+        def bank(number, shape):
+            return ps.tile(shape, F32, name="bank%d" % number)
 
         lists = {}
 
@@ -43,15 +47,15 @@ def tile_picked_triogatebflowbmed_none_po_kernel(
         def entries(name, c0, n):
             return lists[name][:, c0 // 16 : (c0 + n) // 16]
 
-        def load_scale_rows(plane, src):
-            for q in range(4):
+        def load_scale_rows(plane, src, quadrants=range(4)):
+            for q in quadrants:
                 nc.sync.dma_start(plane[32 * q : 32 * q + 4, :].bitcast(I32), src[0, 4 * q : 4 * q + 4, :].bitcast(I32))
 
         xs = new("xs", [P, T], U8)
         nc.vector.memset(xs[:].bitcast(I32), 0)
         ws_raw = {}
         for w in (2, 1, 3, 4):
-            ws_raw[w] = new("ws_raw%d" % w, [P, S], U8)
+            ws_raw[w] = new("ws_raw%d" % w, [P, S], U8, tag="ws_raw%d" % w)
             nc.vector.memset(ws_raw[w][:].bitcast(I32), 0)
 
         warm_in = new("warm_in", [P, 1], F32)
@@ -65,13 +69,14 @@ def tile_picked_triogatebflowbmed_none_po_kernel(
         for w in (2, 1, 3, 4):
             ww_raw[w] = new("ww_raw%d" % w, [P, 2 * S], U8)
             nc.sync.dma_start(ww_raw[w][:].bitcast(I32), w_words[w][0].bitcast(I32))
-        xw = new("xw", [P, T], I32)
-        nc.sync.dma_start(xw[:], x_words[0].rearrange("p n t -> p (n t)").bitcast(I32))
         load_list("two", two)
         load_list("offs", offs)
-        load_list("three", three)
+        load_scale_rows(ws_raw[2], w_scales[2], range(0, 1))
+        xw = new("xw", [P, T], I32)
+        nc.sync.dma_start(xw[:], x_words[0].rearrange("p n t -> p (n t)").bitcast(I32))
         load_scale_rows(xs, x_scales)
-        load_scale_rows(ws_raw[2], w_scales[2])
+        load_scale_rows(ws_raw[2], w_scales[2], range(1, 4))
+        load_list("three", three)
         load_scale_rows(ws_raw[1], w_scales[1])
         load_list("n2", n2)
         load_list("n1", n1)
@@ -113,67 +118,118 @@ def tile_picked_triogatebflowbmed_none_po_kernel(
                 stop=True,
             )
 
-        def pick(name):
-            codes = new("codes_" + name, [P, S], U32)
+        def pick(name, tag=""):
+            codes = new("codes_" + name, [P, S], U32, tag=tag)
             scales = new("scales_" + name, [P, S], U8)
             nc.vector.tensor_copy(codes[:], xw[:].bitcast(U32).indirect(lists[name][:]))
             nc.vector.tensor_copy(scales[:], xs[:].indirect(lists[name][:]))
             return codes, scales
 
-        def project(w, picked):
+        def project(w, picked, first_bank):
             banks = []
             for t in range(R):
-                bank = ps.tile([P, S], F32, name="bank")
-                product(bank[:], w, t, picked[0][:], picked[1][:])
-                banks.append(bank)
+                acc = bank(first_bank + t, [P, S])
+                product(acc[:], w, t, picked[0][:], picked[1][:])
+                banks.append(acc)
             return banks
+
+        ident = new("ident", [P, P], F32)
+        make_identity(nc, ident[:])
+        half_gain = new("half_gain", [P, R], F32)
+        nc.scalar.activation(half_gain[:], gain[:], ACT.Copy, scale=0.5)
 
         for w in (2, 1, 3, 4):
             deal_words(w)
         x_two = pick("two")
         deal_scales(2)
-        d_ps = project(2, x_two)
-        x_offs = pick("offs")
+        d_ps = project(2, x_two, 0)
+        x_offs = pick("offs", "ws_raw2")
         deal_scales(1)
-        y_ps = project(1, x_offs)
-        x_three = pick("three")
+        y_ps = project(1, x_offs, 4)
+        x_three = pick("three", "ws_raw1")
         deal_scales(3)
 
-        def rows(name):
-            return [new("%s%d" % (name, t), [P, S], F32) for t in range(R)]
+        def rows(name, width):
+            return [new("%s%d" % (name, t), [P, width], F32) for t in range(R)]
 
-        d, gate, yh, yg, m1, m1c, bg = (rows(n) for n in ("d", "gate", "yh", "yg", "m1", "m1c", "bg"))
-        u, v, p, w5 = (rows(n) for n in ("u", "v", "p", "w5"))
-        halves = [slice(0, HALF), slice(HALF, S)]
-        z = [new("z%d" % h, [P, R, HALF], F32) for h in range(2)]
+        d, yg, m1, m1c, bg, hw = (rows(n, S) for n in ("d", "yg", "m1", "m1c", "bg", "hw"))
+        yh_gate = rows("yh_gate", 2 * S)
+        u, p, w5 = ([new("%s%d" % (n, h), [P, R, HALF], F32) for h in range(2)] for n in ("u", "p", "w5"))
+        v = {}
 
         def leave_banks(t):
             nc.scalar.copy(d[t][:], d_ps[t][:])
-            for h in range(2):
-                nc.scalar.activation(gate[t][:, halves[h]], d[t][:].indirect(entries("n2", HALF * h, HALF)), ACT.Sigmoid)
-            nc.scalar.activation(yh[t][:], y_ps[t][:], ACT.Copy, scale=-0.5)
+            for c0 in (0, HALF):
+                nc.scalar.activation(yh_gate[t][:, S + c0 : S + c0 + HALF], d[t][:].indirect(entries("n2", c0, HALF)), ACT.Sigmoid)
+            nc.scalar.activation(yh_gate[t][:, 0:S], y_ps[t][:], ACT.Copy, scale=-0.5)
 
         def make_bg(t):
-            bank = ps.tile([P, S], F32, name="bank")
-            product(bank[:], 3, t, x_three[0][:], x_three[1][:])
-            nc.scalar.activation(bg[t][:], bank[:], ACT.Copy, scale=gain[:, t : t + 1])
+            acc = bank(t, [P, S])
+            product(acc[:], 3, t, x_three[0][:], x_three[1][:])
+            nc.scalar.activation(bg[t][:], acc[:], ACT.Copy, scale=half_gain[:, t : t + 1])
 
         def make_yg(t):
-            nc.vector.scalar_tensor_tensor(yg[t][:], yh[t][:], -2.0, gate[t][:], ALU.mult, ALU.mult)
-
-        def fused(dst, window, name, h, other, op):
-            nc.vector.tensor_tensor(dst[:, halves[h]], window[:].indirect(entries(name, HALF * h, HALF)), other[:, halves[h]], op)
+            nc.vector.scalar_tensor_tensor(yg[t][:], yh_gate[t][:, 0:S], -2.0, yh_gate[t][:, S : 2 * S], ALU.mult, ALU.mult)
 
         def make_m1(t):
-            for h in range(2):
-                fused(m1[t], yh[t], "n1", h, yg[t], ALU.add)
+            nc.vector.tensor_tensor(m1[t][:], yh_gate[t][:].indirect(lists["n1"][:]), yg[t][:], ALU.add)
             nc.scalar.copy(m1c[t][:], m1[t][:])
 
-        def make_z(t, h):
-            nc.vector.scalar_tensor_tensor(z[h][:, t, :], w5[t][:, halves[h]], 0.5, p[t][:, halves[h]], ALU.mult, ALU.add)
+        def part(tiles, t, c0, n):
+            return tiles[c0 // HALF][:, t, c0 % HALF : c0 % HALF + n]
+
+        def make_v(t, c0, n, tag=""):
+            v[t, c0] = new("v%d_%d" % (t, c0), [P, n], F32, tag=tag)
+            nc.vector.tensor_tensor(v[t, c0][:], m1[t][:].indirect(entries("n4", c0, n)), m1c[t][:, c0 : c0 + n], ALU.subtract)
+
+        def make_u(t, c0, n):
+            nc.vector.tensor_tensor(part(u, t, c0, n), m1[t][:].indirect(entries("n3", c0, n)), m1c[t][:, c0 : c0 + n], ALU.subtract)
+
+        def make_w(t, c0, n):
+            nc.vector.tensor_tensor(part(w5, t, c0, n), bg[t][:].indirect(entries("n5", c0, n)), v[t, c0][:], ALU.mult)
+
+        def make_p(t, c0, n):
+            nc.vector.scalar_tensor_tensor(part(p, t, c0, n), bg[t][:, c0 : c0 + n], 2.0, part(u, t, c0, n), ALU.mult, ALU.mult)
+
+        def turn_sum(acc, first, second):
+            nc.tensor.matmul(acc, first, ident[:], start=True, stop=False, is_transpose=True)
+            nc.tensor.matmul(acc, second, ident[:], start=False, stop=True, is_transpose=True)
 
         def weave(engine_copy, dst, src):
-            engine_copy(dst[:].rearrange("p (c i) t -> p c t i", i=4), src[:].rearrange("p t (c i) -> p c t i", i=4))
+            engine_copy(dst.rearrange("p (c i) t -> p c t i", i=4), src.rearrange("p t (c i) -> p c t i", i=4))
+
+        z_turned = {}
+
+        def sum_z(t, block):
+            if t == 0:
+                z_turned[block] = bank(4 + block, [P, R, P])
+            turn_sum(z_turned[block][:, t, :], part(p, t, P * block, P), part(w5, t, P * block, P))
+
+        def turn_z_back(block, words_ps, dst):
+            pairs = new("z_pairs%d" % block, [P, 2, P, 2], BF16)
+            nc.scalar.copy(pairs[:], z_turned[block][:].rearrange("q (u e) p -> q u p e", e=2))
+            words = pairs[:].rearrange("q u p e -> q (u p e)").bitcast(F32)
+            for half in range(2):
+                nc.tensor.transpose(words_ps[:, half, :], words[:, P * half : P * (half + 1)], ident[:])
+            nc.scalar.copy(dst.rearrange("p q t -> p (q t)").bitcast(F32).rearrange("p (q u) -> p q u", u=2), words_ps.rearrange("p u q -> p q u"))
+
+        zb = [new("zb%d" % h, [P, HALF, R], BF16, tag="zb%d" % h) for h in range(2)]
+        hc = [new("hc%d" % c, [P, R, n], F32) for c, (c0, n) in enumerate(OUT_CHUNKS)]
+
+        def last_layer(h, numbers):
+            zq = new("zq%d" % h, [P, HALF], U32)
+            zs = new("zs%d" % h, [P, HALF], U8)
+            nc.vector.quantize_mx(out=zq[:].bitcast(FP8X4), scales=zs[:], in_=zb[h][:].rearrange("p c t -> p (c t)"))
+            banks = [bank(number, [P, 2, HALF]) for number in numbers]
+            for t in range(R):
+                product(banks[t // 2][:, t % 2, :], 4, t, zq[:], zs[:])
+            for t in range(R):
+                nc.scalar.copy(hw[t][:, HALF * h : HALF * (h + 1)], banks[t // 2][:, t % 2, :])
+            for c, (c0, n) in enumerate(OUT_CHUNKS):
+                if c0 // HALF == h:
+                    for i, acc in enumerate(banks):
+                        nc.scalar.copy(hc[c][:, 2 * i : 2 * i + 2, :], acc[:, :, c0 % HALF : c0 % HALF + n])
+            return zq
 
         leave_banks(0)
         leave_banks(1)
@@ -181,55 +237,50 @@ def tile_picked_triogatebflowbmed_none_po_kernel(
         deal_scales(4)
         make_m1(0)
         make_bg(0)
-        for t in range(R - 1):
-            make_bg(t + 1)
+        for t in range(R):
+            if t + 1 < R:
+                make_bg(t + 1)
             if t + 2 < R:
                 leave_banks(t + 2)
-            make_yg(t + 1)
-            fused(v[t], m1[t], "n4", 0, m1c[t], ALU.subtract)
-            fused(v[t], m1[t], "n4", 1, m1c[t], ALU.subtract)
-            make_m1(t + 1)
-            fused(u[t], m1[t], "n3", 0, m1c[t], ALU.subtract)
-            fused(u[t], m1[t], "n3", 1, m1c[t], ALU.subtract)
-            fused(w5[t], bg[t], "n5", 0, v[t], ALU.mult)
-            nc.vector.tensor_tensor(p[t][:], u[t][:], bg[t][:], ALU.mult)
-            fused(w5[t], bg[t], "n5", 1, v[t], ALU.mult)
-            make_z(t, 0)
-            make_z(t, 1)
+            if t + 1 < R:
+                make_yg(t + 1)
+            make_v(t, 0, HALF)
+            make_u(t, 0, HALF)
+            if t + 1 < R:
+                make_m1(t + 1)
+            make_w(t, 0, HALF)
+            make_p(t, 0, HALF)
+            sum_z(t, 0)
+            sum_z(t, 1)
 
-        zb = [new("zb%d" % h, [P, HALF, R], BF16) for h in range(2)]
-        zq = [new("zq%d" % h, [P, HALF], U32) for h in range(2)]
-        zs = [new("zs%d" % h, [P, HALF], U8) for h in range(2)]
-        hw = rows("hw")
-        hc = [new("hc%d" % c, [P, R, n], F32) for c, (c0, n) in enumerate(OUT_CHUNKS)]
-
-        def last_layer(h):
-            nc.vector.quantize_mx(out=zq[h][:].bitcast(FP8X4), scales=zs[h][:], in_=zb[h][:].rearrange("p c t -> p (c t)"))
-            banks = [ps.tile([P, 2, HALF], F32, name="bank") for pair in range(2)]
-            for t in range(R):
-                product(banks[t // 2][:, t % 2, :], 4, t, zq[h][:], zs[h][:])
-            for t in range(R):
-                nc.scalar.copy(hw[t][:, halves[h]], banks[t // 2][:, t % 2, :])
-            for c, (c0, n) in enumerate(OUT_CHUNKS):
-                if c0 // HALF == h:
-                    for pair in range(2):
-                        nc.scalar.copy(hc[c][:, 2 * pair : 2 * pair + 2, :], banks[pair][:, :, c0 - HALF * h : c0 - HALF * h + n])
-
+        words01 = bank(7, [P, 2, 2, P])
+        for block in range(2):
+            turn_z_back(block, words01[:, block, :, :], zb[0][:, P * block : P * (block + 1), :])
+        for t in range(R - 1):
+            if t == 2:
+                last_layer(0, (1, 2))
+            make_v(t, HALF, HALF, "zb0" if t == 2 else "")
+            make_u(t, HALF, HALF)
+            make_w(t, HALF, HALF)
+            make_p(t, HALF, HALF)
+            sum_z(t, 2)
+        z_last = new("z_last", [P, R, P], F32)
         t = R - 1
-        fused(v[t], m1[t], "n4", 0, m1c[t], ALU.subtract)
-        fused(u[t], m1[t], "n3", 0, m1c[t], ALU.subtract)
-        fused(w5[t], bg[t], "n5", 0, v[t], ALU.mult)
-        nc.vector.tensor_tensor(p[t][:, halves[0]], u[t][:, halves[0]], bg[t][:, halves[0]], ALU.mult)
-        fused(v[t], m1[t], "n4", 1, m1c[t], ALU.subtract)
-        make_z(t, 0)
-        weave(nc.scalar.copy, zb[0], z[0])
-        fused(u[t], m1[t], "n3", 1, m1c[t], ALU.subtract)
-        fused(w5[t], bg[t], "n5", 1, v[t], ALU.mult)
-        nc.vector.tensor_tensor(p[t][:, halves[1]], u[t][:, halves[1]], bg[t][:, halves[1]], ALU.mult)
-        last_layer(0)
-        make_z(t, 1)
-        weave(nc.vector.tensor_copy, zb[1], z[1])
-        last_layer(1)
+        make_v(t, HALF, P)
+        make_u(t, HALF, P)
+        nc.vector.tensor_tensor(z_last[:, 0:t, :], p[1][:, 0:t, P:HALF], w5[1][:, 0:t, P:HALF], ALU.add)
+        make_w(t, HALF, P)
+        make_p(t, HALF, P)
+        sum_z(t, 2)
+        words2 = bank(0, [P, 2, P])
+        turn_z_back(2, words2[:], zb[1][:, 0:P, :])
+        make_v(t, HALF + P, P)
+        make_u(t, HALF + P, P)
+        make_w(t, HALF + P, P)
+        make_p(t, HALF + P, P)
+        nc.vector.tensor_tensor(z_last[:, t, :], p[1][:, t, P:HALF], w5[1][:, t, P:HALF], ALU.add)
+        weave(nc.vector.tensor_copy, zb[1][:, P:HALF, :], z_last[:])
+        zq_last = last_layer(1, (3, 4))
 
         oq = new("oq", [P, S], U32)
         osc = new("osc", [P, S], U8)
@@ -257,10 +308,22 @@ def tile_picked_triogatebflowbmed_none_po_kernel(
             else:
                 nc.vector.tensor_tensor(flat(res[c], ts), flat(med[c], ts), flat(hc[c], ts), ALU.add)
 
-        def hand_out(c, engine_copy):
+        def add_h(c):
             c0, n = OUT_CHUNKS[c]
+            for b0 in range(0, n, P):
+                block = (c0 + b0) // P
+                cols = slice(b0, b0 + P)
+                turned = bank(5 + block, [P, R, P])
+                for t in range(R):
+                    turn_sum(turned[:, t, :], hc[c][:, t, cols], med[c][:, t, cols])
+                staged = new("staged%d" % block, [P, R, P], F32)
+                nc.scalar.copy(staged[:], turned[:])
+                back = bank(block, [P, R, P])
+                for t in range(R):
+                    nc.tensor.transpose(back[:, t, :], staged[:, t, :], ident[:])
+                nc.scalar.copy(resb[c][:, cols, :], back[:].rearrange("p t q -> p q t"))
+                nc.scalar.copy(res[c][:, :, cols], back[:])
             nc.sync.dma_start(out_rows[:, :, c0 : c0 + n], res[c][:])
-            weave(engine_copy, resb[c], res[c])
 
         def planes(c):
             c0, n = OUT_CHUNKS[c]
@@ -272,17 +335,18 @@ def tile_picked_triogatebflowbmed_none_po_kernel(
         for c in range(last + 1):
             for t in range(R):
                 fetch(c, t)
-                if c > 0 and t < 3:
+                if c > 0 and t < 2:
                     step(c - 1, t, every)
             if c > 0:
-                hand_out(c - 1, nc.scalar.copy)
-            if c > 1:
-                planes(c - 2)
+                add_h(c - 1)
+        planes(0)
         for k in range(3):
             step(last, k, slice(0, 2))
             step(last, k, slice(2, 4))
+        c0, n = OUT_CHUNKS[last]
+        nc.sync.dma_start(out_rows[:, :, c0 : c0 + n], res[last][:])
+        weave(nc.vector.tensor_copy, resb[last][:], res[last][:])
         planes(last - 1)
-        hand_out(last, nc.vector.tensor_copy)
         planes(last)
         for q in range(4):
             queue = nc.scalar if q % 2 else nc.sync

@@ -20,7 +20,8 @@ T = 2048
 S = 512
 HALF = 256
 FLOPS = 4 * 2 * 512 * 512 * 512
-OUT_CHUNKS = ((0, 256), (256, 128), (384, 128))
+MAIN = 384
+WIDE = 768
 
 
 def tile_picked_triogatebflowbmed_none_po_kernel(
@@ -47,8 +48,8 @@ def tile_picked_triogatebflowbmed_none_po_kernel(
         def entries(name, c0, n):
             return lists[name][:, c0 // 16 : (c0 + n) // 16]
 
-        def load_scale_rows(plane, src, quadrants=range(4)):
-            for q in quadrants:
+        def load_scale_rows(plane, src):
+            for q in range(4):
                 nc.sync.dma_start(plane[32 * q : 32 * q + 4, :].bitcast(I32), src[0, 4 * q : 4 * q + 4, :].bitcast(I32))
 
         xs = new("xs", [P, T], U8)
@@ -66,26 +67,31 @@ def tile_picked_triogatebflowbmed_none_po_kernel(
         w_words = {1: w1_words, 2: w2_words, 3: w3_words, 4: w4_words}
         w_scales = {1: w1_scales, 2: w2_scales, 3: w3_scales, 4: w4_scales}
         ww_raw = {}
-        for w in (2, 1, 3, 4):
+
+        def load_words(w):
             ww_raw[w] = new("ww_raw%d" % w, [P, 2 * S], U8)
             nc.sync.dma_start(ww_raw[w][:].bitcast(I32), w_words[w][0].bitcast(I32))
+
+        load_words(2)
+        load_words(1)
         load_list("two", two)
-        load_list("offs", offs)
-        load_scale_rows(ws_raw[2], w_scales[2], range(0, 1))
+        load_scale_rows(xs, x_scales)
         xw = new("xw", [P, T], I32)
         nc.sync.dma_start(xw[:], x_words[0].rearrange("p n t -> p (n t)").bitcast(I32))
-        load_scale_rows(xs, x_scales)
-        load_scale_rows(ws_raw[2], w_scales[2], range(1, 4))
+        load_scale_rows(ws_raw[2], w_scales[2])
+        load_list("offs", offs)
+        load_list("n2", n2)
         load_list("three", three)
         load_scale_rows(ws_raw[1], w_scales[1])
-        load_list("n2", n2)
+        load_words(3)
         load_list("n1", n1)
-        load_scale_rows(ws_raw[3], w_scales[3])
         gain = new("gain", [P, R], F32)
         nc.sync.dma_start(gain[:], gn.rearrange("(p t) o -> p (t o)", t=R))
+        load_scale_rows(ws_raw[3], w_scales[3])
         load_list("n4", n4)
         load_list("n3", n3)
         load_list("n5", n5)
+        load_words(4)
         load_scale_rows(ws_raw[4], w_scales[4])
         load_list("n6", n6)
         load_list("n7", n7)
@@ -93,15 +99,15 @@ def tile_picked_triogatebflowbmed_none_po_kernel(
         ww = {}
         ws = {}
 
-        def deal_words(w):
-            ww[w] = new("ww%d" % w, [P, 2 * S], U8)
+        def deal_words(w, tag=""):
+            ww[w] = new("ww%d" % w, [P, 2 * S], U8, tag=tag)
             nc.vector.tensor_copy(
                 ww[w][:].rearrange("p (t m b) -> p t m b", t=R, b=2),
                 ww_raw[w][:].rearrange("p (m t b) -> p t m b", t=R, b=2),
             )
 
-        def deal_scales(w):
-            ws[w] = new("ws%d" % w, [P, S], U8)
+        def deal_scales(w, tag=""):
+            ws[w] = new("ws%d" % w, [P, S], U8, tag=tag)
             nc.vector.tensor_copy(
                 ws[w][:].rearrange("p (t m) -> p t m", t=R),
                 ws_raw[w][:].rearrange("p (m t) -> p t m", t=R),
@@ -121,75 +127,69 @@ def tile_picked_triogatebflowbmed_none_po_kernel(
         def pick(name, tag=""):
             codes = new("codes_" + name, [P, S], U32, tag=tag)
             scales = new("scales_" + name, [P, S], U8)
-            nc.vector.tensor_copy(codes[:], xw[:].bitcast(U32).indirect(lists[name][:]))
             nc.vector.tensor_copy(scales[:], xs[:].indirect(lists[name][:]))
+            nc.vector.tensor_copy(codes[:], xw[:].bitcast(U32).indirect(lists[name][:]))
             return codes, scales
 
-        def project(w, picked, first_bank):
-            banks = []
-            for t in range(R):
-                acc = bank(first_bank + t, [P, S])
-                product(acc[:], w, t, picked[0][:], picked[1][:])
-                banks.append(acc)
-            return banks
+        def project(w, t, picked, number):
+            acc = bank(number, [P, S])
+            product(acc[:], w, t, picked[0][:], picked[1][:])
+            return acc
 
         ident = new("ident", [P, P], F32)
         make_identity(nc, ident[:])
         half_gain = new("half_gain", [P, R], F32)
         nc.scalar.activation(half_gain[:], gain[:], ACT.Copy, scale=0.5)
 
-        for w in (2, 1, 3, 4):
-            deal_words(w)
+        def rows(name, width):
+            return [new("%s%d" % (name, t), [P, width], F32, tag="%s%d" % (name, t)) for t in range(R)]
+
+        m1, hw = rows("m1_", WIDE), rows("hw", WIDE)
+        for tile in m1 + hw:
+            nc.gpsimd.memset(tile[:, S:WIDE], 0.0)
+
+        deal_words(2)
+        deal_words(1)
         x_two = pick("two")
         deal_scales(2)
-        d_ps = project(2, x_two, 0)
+        d_ps = {t: project(2, t, x_two, t) for t in range(2)}
         x_offs = pick("offs", "ws_raw2")
         deal_scales(1)
-        y_ps = project(1, x_offs, 4)
+        y_ps = [project(1, t, x_offs, 4 + t) for t in range(R)]
         x_three = pick("three", "ws_raw1")
+        deal_words(3)
         deal_scales(3)
 
-        def rows(name, width):
-            return [new("%s%d" % (name, t), [P, width], F32) for t in range(R)]
-
-        d, yg, m1, m1c, bg, hw = (rows(n, S) for n in ("d", "yg", "m1", "m1c", "bg", "hw"))
+        d, yg, m1c, bg, hc = (rows(n, S) for n in ("d", "yg", "m1c", "bg", "hc"))
         yh_gate = rows("yh_gate", 2 * S)
-        u, p, w5 = ([new("%s%d" % (n, h), [P, R, HALF], F32) for h in range(2)] for n in ("u", "p", "w5"))
-        v = {}
+        main, rest = slice(0, MAIN), slice(MAIN, S)
+        u, v, p, w5 = (rows(n, MAIN) for n in ("u", "v", "p", "w5_"))
+        u_r, p_r, w_r = (new(n, [P, R, P], F32) for n in ("u_r", "p_r", "w_r"))
 
         def leave_banks(t):
+            if t not in d_ps:
+                d_ps[t] = project(2, t, x_two, 2 + t)
             nc.scalar.copy(d[t][:], d_ps[t][:])
             for c0 in (0, HALF):
                 nc.scalar.activation(yh_gate[t][:, S + c0 : S + c0 + HALF], d[t][:].indirect(entries("n2", c0, HALF)), ACT.Sigmoid)
             nc.scalar.activation(yh_gate[t][:, 0:S], y_ps[t][:], ACT.Copy, scale=-0.5)
 
         def make_bg(t):
-            acc = bank(t, [P, S])
-            product(acc[:], 3, t, x_three[0][:], x_three[1][:])
+            acc = project(3, t, x_three, t % 2)
             nc.scalar.activation(bg[t][:], acc[:], ACT.Copy, scale=half_gain[:, t : t + 1])
 
         def make_yg(t):
             nc.vector.scalar_tensor_tensor(yg[t][:], yh_gate[t][:, 0:S], -2.0, yh_gate[t][:, S : 2 * S], ALU.mult, ALU.mult)
 
         def make_m1(t):
-            nc.vector.tensor_tensor(m1[t][:], yh_gate[t][:].indirect(lists["n1"][:]), yg[t][:], ALU.add)
-            nc.scalar.copy(m1c[t][:], m1[t][:])
+            nc.vector.tensor_tensor(m1[t][:, 0:S], yh_gate[t][:].indirect(lists["n1"][:]), yg[t][:], ALU.add)
+            nc.scalar.copy(m1c[t][:], m1[t][:, 0:S])
 
-        def part(tiles, t, c0, n):
-            return tiles[c0 // HALF][:, t, c0 % HALF : c0 % HALF + n]
+        def fetch(dst, window, name, cols, other, op):
+            nc.vector.tensor_tensor(dst, window[:].indirect(lists[name][:, cols.start // 16 : cols.stop // 16]), other, op)
 
-        def make_v(t, c0, n, tag=""):
-            v[t, c0] = new("v%d_%d" % (t, c0), [P, n], F32, tag=tag)
-            nc.vector.tensor_tensor(v[t, c0][:], m1[t][:].indirect(entries("n4", c0, n)), m1c[t][:, c0 : c0 + n], ALU.subtract)
-
-        def make_u(t, c0, n):
-            nc.vector.tensor_tensor(part(u, t, c0, n), m1[t][:].indirect(entries("n3", c0, n)), m1c[t][:, c0 : c0 + n], ALU.subtract)
-
-        def make_w(t, c0, n):
-            nc.vector.tensor_tensor(part(w5, t, c0, n), bg[t][:].indirect(entries("n5", c0, n)), v[t, c0][:], ALU.mult)
-
-        def make_p(t, c0, n):
-            nc.vector.scalar_tensor_tensor(part(p, t, c0, n), bg[t][:, c0 : c0 + n], 2.0, part(u, t, c0, n), ALU.mult, ALU.mult)
+        def make_p(dst, t, cols, diff):
+            nc.vector.scalar_tensor_tensor(dst, bg[t][:, cols], 2.0, diff, ALU.mult, ALU.mult)
 
         def turn_sum(acc, first, second):
             nc.tensor.matmul(acc, first, ident[:], start=True, stop=False, is_transpose=True)
@@ -198,43 +198,34 @@ def tile_picked_triogatebflowbmed_none_po_kernel(
         def weave(engine_copy, dst, src):
             engine_copy(dst.rearrange("p (c i) t -> p c t i", i=4), src.rearrange("p t (c i) -> p c t i", i=4))
 
-        z_turned = {}
+        blocks = [slice(P * i, P * (i + 1)) for i in range(MAIN // P)]
+        z_turned = []
 
-        def sum_z(t, block):
-            if t == 0:
-                z_turned[block] = bank(4 + block, [P, R, P])
-            turn_sum(z_turned[block][:, t, :], part(p, t, P * block, P), part(w5, t, P * block, P))
+        def sum_z(t):
+            for i, cols in enumerate(blocks):
+                if t == 0:
+                    z_turned.append(bank((2, 3, 6)[i], [P, R, P]))
+                turn_sum(z_turned[i][:, t, :], p[t][:, cols], w5[t][:, cols])
 
-        def turn_z_back(block, words_ps, dst):
-            pairs = new("z_pairs%d" % block, [P, 2, P, 2], BF16)
-            nc.scalar.copy(pairs[:], z_turned[block][:].rearrange("q (u e) p -> q u p e", e=2))
+        def turn_z_back(i, words_ps, dst):
+            pairs = new("z_pairs%d" % i, [P, 2, P, 2], BF16)
+            nc.scalar.copy(pairs[:], z_turned[i][:].rearrange("q (u e) p -> q u p e", e=2))
             words = pairs[:].rearrange("q u p e -> q (u p e)").bitcast(F32)
             for half in range(2):
                 nc.tensor.transpose(words_ps[:, half, :], words[:, P * half : P * (half + 1)], ident[:])
             nc.scalar.copy(dst.rearrange("p q t -> p (q t)").bitcast(F32).rearrange("p (q u) -> p q u", u=2), words_ps.rearrange("p u q -> p q u"))
 
-        zb = [new("zb%d" % h, [P, HALF, R], BF16, tag="zb%d" % h) for h in range(2)]
-        hc = [new("hc%d" % c, [P, R, n], F32) for c, (c0, n) in enumerate(OUT_CHUNKS)]
-
-        def last_layer(h, numbers):
-            zq = new("zq%d" % h, [P, HALF], U32)
-            zs = new("zs%d" % h, [P, HALF], U8)
-            nc.vector.quantize_mx(out=zq[:].bitcast(FP8X4), scales=zs[:], in_=zb[h][:].rearrange("p c t -> p (c t)"))
-            banks = [bank(number, [P, 2, HALF]) for number in numbers]
+        def last_layer(name, woven, n, outs):
+            zq = new("zq" + name, [P, n], U32)
+            zs = new("zs" + name, [P, n], U8)
+            nc.vector.quantize_mx(out=zq[:].bitcast(FP8X4), scales=zs[:], in_=woven[:].rearrange("p c t -> p (c t)"))
             for t in range(R):
-                product(banks[t // 2][:, t % 2, :], 4, t, zq[:], zs[:])
-            for t in range(R):
-                nc.scalar.copy(hw[t][:, HALF * h : HALF * (h + 1)], banks[t // 2][:, t % 2, :])
-            for c, (c0, n) in enumerate(OUT_CHUNKS):
-                if c0 // HALF == h:
-                    for i, acc in enumerate(banks):
-                        nc.scalar.copy(hc[c][:, 2 * i : 2 * i + 2, :], acc[:, :, c0 % HALF : c0 % HALF + n])
+                product(outs[t], 4, t, zq[:], zs[:])
             return zq
 
         leave_banks(0)
         leave_banks(1)
         make_yg(0)
-        deal_scales(4)
         make_m1(0)
         make_bg(0)
         for t in range(R):
@@ -244,110 +235,121 @@ def tile_picked_triogatebflowbmed_none_po_kernel(
                 leave_banks(t + 2)
             if t + 1 < R:
                 make_yg(t + 1)
-            make_v(t, 0, HALF)
-            make_u(t, 0, HALF)
+            fetch(v[t][:], m1[t], "n4", main, m1c[t][:, main], ALU.subtract)
+            fetch(u[t][:], m1[t], "n3", main, m1c[t][:, main], ALU.subtract)
             if t + 1 < R:
                 make_m1(t + 1)
-            make_w(t, 0, HALF)
-            make_p(t, 0, HALF)
-            sum_z(t, 0)
-            sum_z(t, 1)
+            fetch(w5[t][:], bg[t], "n5", main, v[t][:], ALU.mult)
+            make_p(p[t][:], t, main, u[t][:])
+            sum_z(t)
 
-        words01 = bank(7, [P, 2, 2, P])
-        for block in range(2):
-            turn_z_back(block, words01[:, block, :, :], zb[0][:, P * block : P * (block + 1), :])
-        for t in range(R - 1):
-            if t == 2:
-                last_layer(0, (1, 2))
-            make_v(t, HALF, HALF, "zb0" if t == 2 else "")
-            make_u(t, HALF, HALF)
-            make_w(t, HALF, HALF)
-            make_p(t, HALF, HALF)
-            sum_z(t, 2)
-        z_last = new("z_last", [P, R, P], F32)
-        t = R - 1
-        make_v(t, HALF, P)
-        make_u(t, HALF, P)
-        nc.vector.tensor_tensor(z_last[:, 0:t, :], p[1][:, 0:t, P:HALF], w5[1][:, 0:t, P:HALF], ALU.add)
-        make_w(t, HALF, P)
-        make_p(t, HALF, P)
-        sum_z(t, 2)
-        words2 = bank(0, [P, 2, P])
-        turn_z_back(2, words2[:], zb[1][:, 0:P, :])
-        make_v(t, HALF + P, P)
-        make_u(t, HALF + P, P)
-        make_w(t, HALF + P, P)
-        make_p(t, HALF + P, P)
-        nc.vector.tensor_tensor(z_last[:, t, :], p[1][:, t, P:HALF], w5[1][:, t, P:HALF], ALU.add)
-        weave(nc.vector.tensor_copy, zb[1][:, P:HALF, :], z_last[:])
-        zq_last = last_layer(1, (3, 4))
+        deal_words(4, "v%d" % (R - 1))
+        deal_scales(4, "u%d" % (R - 1))
+        zb_a = new("zb_a", [P, HALF, R], BF16, tag="zb_a")
+        zb_b = new("zb_b", [P, P, R], BF16, tag="zb_b")
+        zb_r = new("zb_r", [P, P, R], BF16)
+        words_a = bank(7, [P, 2, 2, P])
+        words_b = bank(0, [P, 2, P])
+        turn_z_back(0, words_a[:, 0, :, :], zb_a[:, 0:P, :])
+        turn_z_back(1, words_a[:, 1, :, :], zb_a[:, P:HALF, :])
+        turn_z_back(2, words_b[:], zb_b[:])
+        h_ps = [bank(number, [P, MAIN]) for number in (1, 4, 5, 7)]
+
+        def leave_h(t):
+            nc.scalar.copy(hw[t][:, main], h_ps[t][:])
+            nc.scalar.copy(hc[t][:, main], h_ps[t][:])
+
+        for t in range(R):
+            if t == R - 1:
+                last_layer("a", zb_a, HALF, [h_ps[i][:, 0:HALF] for i in range(R)])
+            v_r = new("v_r%d" % t, [P, P], F32, tag="zb_a" if t == R - 1 else "")
+            fetch(v_r[:], m1c[t], "n4", rest, m1[t][:, rest], ALU.subtract)
+            fetch(u_r[:, t, :], m1c[t], "n3", rest, m1[t][:, rest], ALU.subtract)
+            if t == R - 1:
+                last_layer("b", zb_b, P, [h_ps[i][:, HALF:MAIN] for i in range(R)])
+                z_r = new("z_r", [P, R, P], F32, tag="zb_b")
+                nc.vector.tensor_tensor(z_r[:, 0:t, :], p_r[:, 0:t, :], w_r[:, 0:t, :], ALU.add)
+            fetch(w_r[:, t, :], bg[t], "n5", rest, v_r[:], ALU.mult)
+            make_p(p_r[:, t, :], t, rest, u_r[:, t, :])
+        nc.vector.tensor_tensor(z_r[:, R - 1, :], p_r[:, R - 1, :], w_r[:, R - 1, :], ALU.add)
+        weave(nc.vector.tensor_copy, zb_r[:], z_r[:])
+        leave_h(0)
+        leave_h(1)
+        h_r = [bank(number, [P, 2, P]) for number in (0, 6)]
+        zq_last = last_layer("r", zb_r, P, [h_r[i // 2][:, i % 2, :] for i in range(R)])
+        for t in range(R):
+            if t > 1:
+                leave_h(t)
+            leave = nc.vector.tensor_copy if t == 0 else nc.scalar.copy
+            leave(hw[t][:, rest], h_r[t // 2][:, t % 2, :])
+        for t in range(R):
+            nc.scalar.copy(hc[t][:, rest], h_r[t // 2][:, t % 2, :])
 
         oq = new("oq", [P, S], U32)
         osc = new("osc", [P, S], U8)
         out_rows = out_0.rearrange("(p t) s -> p t s", t=R)
         out_words = out_1[0].rearrange("p n t -> p (n t)").bitcast(I32)
-        da, db, lo, med, res = (
-            [new("%s%d" % (name, c), [P, R, n], F32) for c, (c0, n) in enumerate(OUT_CHUNKS)]
-            for name in ("da", "db", "lo", "med", "res")
-        )
-        resb = [new("resb%d" % c, [P, n, R], BF16) for c, (c0, n) in enumerate(OUT_CHUNKS)]
+        da, db, lo, med = (rows(n, MAIN) for n in ("da", "db", "lo", "med"))
+        da_r, db_r, lo_r, med_r, res_r = (new(n, [P, R, P], F32) for n in ("da_r", "db_r", "lo_r", "med_r", "res_r"))
+        res = new("res", [P, R, MAIN], F32)
 
-        def fetch(c, t):
-            c0, n = OUT_CHUNKS[c]
-            nc.vector.tensor_tensor(da[c][:, t, :], hw[t][:].indirect(entries("n6", c0, n)), hc[c][:, t, :], ALU.subtract)
-            nc.vector.tensor_tensor(db[c][:, t, :], hw[t][:].indirect(entries("n7", c0, n)), hc[c][:, t, :], ALU.subtract)
+        def clip_above(dst, first, second):
+            nc.vector.scalar_tensor_tensor(dst, first, 0.0, second, ALU.max, ALU.min)
 
-        def flat(tile, ts):
-            return tile[:, ts, :].rearrange("p t n -> p (t n)")
+        def clip_below(dst, first, clipped):
+            nc.vector.scalar_tensor_tensor(dst, first, 0.0, clipped, ALU.min, ALU.max)
 
-        def step(c, k, ts):
-            if k == 0:
-                nc.vector.scalar_tensor_tensor(flat(lo[c], ts), flat(da[c], ts), 0.0, flat(db[c], ts), ALU.max, ALU.min)
-            elif k == 1:
-                nc.vector.scalar_tensor_tensor(flat(med[c], ts), flat(da[c], ts), 0.0, flat(lo[c], ts), ALU.min, ALU.max)
+        def add_h(t):
+            turned = bank(2 + t % 2, [P, MAIN])
+            for cols in blocks:
+                turn_sum(turned[:, cols], hc[t][:, cols], med[t][:, cols])
+            staged = new("staged%d" % t, [P, MAIN], F32)
+            nc.scalar.copy(staged[:], turned[:])
+            back = bank((1, 4, 5, 7)[t], [P, MAIN])
+            for cols in blocks:
+                nc.tensor.transpose(back[:, cols], staged[:, cols], ident[:])
+            nc.scalar.copy(res[:, t, :], back[:])
+            nc.sync.dma_start(out_rows[:, t, main], res[:, t, :])
+
+        def planes(woven, cols):
+            nc.vector.quantize_mx(out=oq[:, cols].bitcast(FP8X4), scales=osc[:, cols], in_=woven[:].rearrange("p c t -> p (c t)"))
+
+        for t in range(R + 1):
+            if t < R:
+                fetch(da[t][:], hw[t], "n6", main, hc[t][:, main], ALU.subtract)
             else:
-                nc.vector.tensor_tensor(flat(res[c], ts), flat(med[c], ts), flat(hc[c], ts), ALU.add)
-
-        def add_h(c):
-            c0, n = OUT_CHUNKS[c]
-            for b0 in range(0, n, P):
-                block = (c0 + b0) // P
-                cols = slice(b0, b0 + P)
-                turned = bank(5 + block, [P, R, P])
-                for t in range(R):
-                    turn_sum(turned[:, t, :], hc[c][:, t, cols], med[c][:, t, cols])
-                staged = new("staged%d" % block, [P, R, P], F32)
-                nc.scalar.copy(staged[:], turned[:])
-                back = bank(block, [P, R, P])
-                for t in range(R):
-                    nc.tensor.transpose(back[:, t, :], staged[:, t, :], ident[:])
-                nc.scalar.copy(resb[c][:, cols, :], back[:].rearrange("p t q -> p q t"))
-                nc.scalar.copy(res[c][:, :, cols], back[:])
-            nc.sync.dma_start(out_rows[:, :, c0 : c0 + n], res[c][:])
-
-        def planes(c):
-            c0, n = OUT_CHUNKS[c]
-            nc.vector.quantize_mx(out=oq[:, c0 : c0 + n].bitcast(FP8X4), scales=osc[:, c0 : c0 + n], in_=resb[c][:].rearrange("p c t -> p (c t)"))
-            nc.sync.dma_start(out_words[:, c0 : c0 + n], oq[:, c0 : c0 + n].bitcast(I32))
-
-        every = slice(0, R)
-        last = len(OUT_CHUNKS) - 1
-        for c in range(last + 1):
-            for t in range(R):
-                fetch(c, t)
-                if c > 0 and t < 2:
-                    step(c - 1, t, every)
-            if c > 0:
-                add_h(c - 1)
-        planes(0)
-        for k in range(3):
-            step(last, k, slice(0, 2))
-            step(last, k, slice(2, 4))
-        c0, n = OUT_CHUNKS[last]
-        nc.sync.dma_start(out_rows[:, :, c0 : c0 + n], res[last][:])
-        weave(nc.vector.tensor_copy, resb[last][:], res[last][:])
-        planes(last - 1)
-        planes(last)
+                fetch(da_r[:, 0, :], hc[0], "n6", rest, hw[0][:, rest], ALU.subtract)
+            if t > 0:
+                clip_above(lo[t - 1][:], da[t - 1][:], db[t - 1][:])
+            if t < R:
+                fetch(db[t][:], hw[t], "n7", main, hc[t][:, main], ALU.subtract)
+            else:
+                fetch(db_r[:, 0, :], hc[0], "n7", rest, hw[0][:, rest], ALU.subtract)
+            if t > 0:
+                clip_below(med[t - 1][:], da[t - 1][:], lo[t - 1][:])
+                add_h(t - 1)
+        resb_a = new("resb_a", [P, HALF, R], BF16)
+        resb_b = new("resb_b", [P, P, R], BF16)
+        resb_r = new("resb_r", [P, P, R], BF16)
+        weave(nc.scalar.copy, resb_a[:], res[:, :, 0:HALF])
+        weave(nc.scalar.copy, resb_b[:], res[:, :, HALF:MAIN])
+        for t in range(1, R):
+            fetch(da_r[:, t, :], hc[t], "n6", rest, hw[t][:, rest], ALU.subtract)
+            fetch(db_r[:, t, :], hc[t], "n7", rest, hw[t][:, rest], ALU.subtract)
+        pairs_of_t = (slice(0, 2), slice(2, 4))
+        for ts in pairs_of_t:
+            clip_above(lo_r[:, ts, :], da_r[:, ts, :], db_r[:, ts, :])
+        for ts in pairs_of_t:
+            clip_below(med_r[:, ts, :], da_r[:, ts, :], lo_r[:, ts, :])
+        for ts, acc in zip(pairs_of_t, h_r):
+            nc.vector.tensor_tensor(res_r[:, ts, :], med_r[:, ts, :], acc[:], ALU.add)
+        nc.sync.dma_start(out_rows[:, :, rest], res_r[:])
+        planes(resb_a, slice(0, HALF))
+        weave(nc.vector.tensor_copy, resb_r[:], res_r[:])
+        planes(resb_b, slice(HALF, MAIN))
+        nc.sync.dma_start(out_words[:, main], oq[:, main].bitcast(I32))
+        planes(resb_r, rest)
+        nc.sync.dma_start(out_words[:, rest], oq[:, rest].bitcast(I32))
         for q in range(4):
             queue = nc.scalar if q % 2 else nc.sync
             queue.dma_start(out_2[0, 4 * q : 4 * q + 4, :].bitcast(I32), osc[32 * q : 32 * q + 4, :].bitcast(I32))

@@ -18,10 +18,20 @@ P = 128
 R = 4
 T = 2048
 S = 512
-HALF = 256
+HALF = S // 2
+MAIN = 3 * P
+WIDE = 2 * MAIN
+PER_COLUMN = 16
 FLOPS = 4 * 2 * 512 * 512 * 512
-MAIN = 384
-WIDE = 768
+
+D_BANKS = (0, 1, 4, 5)
+Y_BANKS = (4, 5, 6, 7)
+B_BANKS = (0, 1, 0, 1)
+Z_SUM_BANKS = (2, 3, 6)
+Z_WORD_BANKS = (7, 0)
+H_BANKS = (1, 4, 5, 7)
+H_REST_BANKS = (0, 6)
+OUT_SUM_BANKS = (2, 3)
 
 
 def tile_picked_triogatebflowbmed_none_po_kernel(
@@ -36,28 +46,31 @@ def tile_picked_triogatebflowbmed_none_po_kernel(
         def new(name, shape, dtype, tag=""):
             return sb.tile(shape, dtype, name=name, tag=tag, align_bytes=64)
 
+        def four(name, width):
+            return [new("%s%d" % (name, t), [P, width], F32, tag="%s%d" % (name, t)) for t in range(R)]
+
         def bank(number, shape):
             return ps.tile(shape, F32, name="bank%d" % number)
 
         lists = {}
 
         def load_list(name, src):
-            lists[name] = new("list_" + name, [P, S // 16], U16)
+            lists[name] = new("list_" + name, [P, S // PER_COLUMN], U16)
             nc.sync.dma_start(lists[name][:], src)
 
-        def entries(name, c0, n):
-            return lists[name][:, c0 // 16 : (c0 + n) // 16]
+        def looked_up(window, name, cols):
+            return window[:].indirect(lists[name][:, cols.start // PER_COLUMN : cols.stop // PER_COLUMN])
 
-        def load_scale_rows(plane, src):
+        def load_scale_rows(dst, src):
             for q in range(4):
-                nc.sync.dma_start(plane[32 * q : 32 * q + 4, :].bitcast(I32), src[0, 4 * q : 4 * q + 4, :].bitcast(I32))
+                nc.sync.dma_start(dst[32 * q : 32 * q + 4, :].bitcast(I32), src[0, 4 * q : 4 * q + 4, :].bitcast(I32))
 
-        xs = new("xs", [P, T], U8)
-        nc.vector.memset(xs[:].bitcast(I32), 0)
-        ws_raw = {}
+        x_scale_rows = new("x_scale_rows", [P, T], U8)
+        nc.vector.memset(x_scale_rows[:].bitcast(I32), 0)
+        raw_scales = {}
         for w in (2, 1, 3, 4):
-            ws_raw[w] = new("ws_raw%d" % w, [P, S], U8, tag="ws_raw%d" % w)
-            nc.vector.memset(ws_raw[w][:].bitcast(I32), 0)
+            raw_scales[w] = new("raw_scales%d" % w, [P, S], U8, tag="raw_scales%d" % w)
+            nc.vector.memset(raw_scales[w][:].bitcast(I32), 0)
 
         warm_in = new("warm_in", [P, 1], F32)
         warm_out = new("warm_out", [P, 1], F32)
@@ -66,58 +79,58 @@ def tile_picked_triogatebflowbmed_none_po_kernel(
 
         w_words = {1: w1_words, 2: w2_words, 3: w3_words, 4: w4_words}
         w_scales = {1: w1_scales, 2: w2_scales, 3: w3_scales, 4: w4_scales}
-        ww_raw = {}
+        raw_words = {}
 
         def load_words(w):
-            ww_raw[w] = new("ww_raw%d" % w, [P, 2 * S], U8)
-            nc.sync.dma_start(ww_raw[w][:].bitcast(I32), w_words[w][0].bitcast(I32))
+            raw_words[w] = new("raw_words%d" % w, [P, 2 * S], U8)
+            nc.sync.dma_start(raw_words[w][:].bitcast(I32), w_words[w][0].bitcast(I32))
 
         load_words(2)
-        load_words(1)
         load_list("two", two)
-        load_scale_rows(xs, x_scales)
-        xw = new("xw", [P, T], I32)
-        nc.sync.dma_start(xw[:], x_words[0].rearrange("p n t -> p (n t)").bitcast(I32))
-        load_scale_rows(ws_raw[2], w_scales[2])
         load_list("offs", offs)
+        load_scale_rows(x_scale_rows, x_scales)
+        x_table = new("x_table", [P, T], I32)
+        nc.sync.dma_start(x_table[:], x_words[0].rearrange("p n t -> p (n t)").bitcast(I32))
+        load_scale_rows(raw_scales[2], w_scales[2])
+        load_words(1)
         load_list("n2", n2)
+        load_scale_rows(raw_scales[1], w_scales[1])
         load_list("three", three)
-        load_scale_rows(ws_raw[1], w_scales[1])
         load_words(3)
         load_list("n1", n1)
         gain = new("gain", [P, R], F32)
         nc.sync.dma_start(gain[:], gn.rearrange("(p t) o -> p (t o)", t=R))
-        load_scale_rows(ws_raw[3], w_scales[3])
+        load_scale_rows(raw_scales[3], w_scales[3])
         load_list("n4", n4)
         load_list("n3", n3)
         load_list("n5", n5)
         load_words(4)
-        load_scale_rows(ws_raw[4], w_scales[4])
+        load_scale_rows(raw_scales[4], w_scales[4])
         load_list("n6", n6)
         load_list("n7", n7)
 
-        ww = {}
-        ws = {}
+        dealt_words = {}
+        dealt_scales = {}
 
         def deal_words(w, tag=""):
-            ww[w] = new("ww%d" % w, [P, 2 * S], U8, tag=tag)
+            dealt_words[w] = new("dealt_words%d" % w, [P, 2 * S], U8, tag=tag)
             nc.vector.tensor_copy(
-                ww[w][:].rearrange("p (t m b) -> p t m b", t=R, b=2),
-                ww_raw[w][:].rearrange("p (m t b) -> p t m b", t=R, b=2),
+                dealt_words[w][:].rearrange("p (t m b) -> p t m b", t=R, b=2),
+                raw_words[w][:].rearrange("p (m t b) -> p t m b", t=R, b=2),
             )
 
         def deal_scales(w, tag=""):
-            ws[w] = new("ws%d" % w, [P, S], U8, tag=tag)
+            dealt_scales[w] = new("dealt_scales%d" % w, [P, S], U8, tag=tag)
             nc.vector.tensor_copy(
-                ws[w][:].rearrange("p (t m) -> p t m", t=R),
-                ws_raw[w][:].rearrange("p (m t) -> p t m", t=R),
+                dealt_scales[w][:].rearrange("p (t m) -> p t m", t=R),
+                raw_scales[w][:].rearrange("p (m t) -> p t m", t=R),
             )
 
         def product(acc, w, t, codes, scales):
             nc.tensor.matmul_mx(
                 out=acc,
-                lhsT=ww[w][:, 2 * P * t : 2 * P * (t + 1)].bitcast(FP4X4),
-                lhsT_scale=ws[w][:, P * t : P * (t + 1)],
+                lhsT=dealt_words[w][:, 2 * P * t : 2 * P * (t + 1)].bitcast(FP4X4),
+                lhsT_scale=dealt_scales[w][:, P * t : P * (t + 1)],
                 rhs=codes.bitcast(FP8X4),
                 rhs_scale=scales,
                 start=True,
@@ -127,8 +140,8 @@ def tile_picked_triogatebflowbmed_none_po_kernel(
         def pick(name, tag=""):
             codes = new("codes_" + name, [P, S], U32, tag=tag)
             scales = new("scales_" + name, [P, S], U8)
-            nc.vector.tensor_copy(scales[:], xs[:].indirect(lists[name][:]))
-            nc.vector.tensor_copy(codes[:], xw[:].bitcast(U32).indirect(lists[name][:]))
+            nc.vector.tensor_copy(scales[:], x_scale_rows[:].indirect(lists[name][:]))
+            nc.vector.tensor_copy(codes[:], x_table[:].bitcast(U32).indirect(lists[name][:]))
             return codes, scales
 
         def project(w, t, picked, number):
@@ -141,55 +154,53 @@ def tile_picked_triogatebflowbmed_none_po_kernel(
         half_gain = new("half_gain", [P, R], F32)
         nc.scalar.activation(half_gain[:], gain[:], ACT.Copy, scale=0.5)
 
-        def rows(name, width):
-            return [new("%s%d" % (name, t), [P, width], F32, tag="%s%d" % (name, t)) for t in range(R)]
-
-        m1, hw = rows("m1_", WIDE), rows("hw", WIDE)
-        for tile in m1 + hw:
-            nc.gpsimd.memset(tile[:, S:WIDE], 0.0)
+        m1_wide, h_wide = four("m1_wide", WIDE), four("h_wide", WIDE)
+        for window in m1_wide + h_wide:
+            nc.gpsimd.memset(window[:, S:WIDE], 0.0)
 
         deal_words(2)
-        deal_words(1)
         x_two = pick("two")
         deal_scales(2)
-        d_ps = {t: project(2, t, x_two, t) for t in range(2)}
-        x_offs = pick("offs", "ws_raw2")
+        d_ps = {t: project(2, t, x_two, D_BANKS[t]) for t in range(2)}
+        x_offs = pick("offs", "raw_scales2")
+        deal_words(1)
         deal_scales(1)
-        y_ps = [project(1, t, x_offs, 4 + t) for t in range(R)]
-        x_three = pick("three", "ws_raw1")
+        y_ps = [project(1, t, x_offs, Y_BANKS[t]) for t in range(R)]
+        x_three = pick("three", "raw_scales1")
         deal_words(3)
         deal_scales(3)
 
-        d, yg, m1c, bg, hc = (rows(n, S) for n in ("d", "yg", "m1c", "bg", "hc"))
-        yh_gate = rows("yh_gate", 2 * S)
+        d, y_gated, m1, bh, h = (four(n, S) for n in ("d", "y_gated", "m1", "bh", "h"))
+        yh_gate = four("yh_gate", 2 * S)
         main, rest = slice(0, MAIN), slice(MAIN, S)
-        u, v, p, w5 = (rows(n, MAIN) for n in ("u", "v", "p", "w5_"))
-        u_r, p_r, w_r = (new(n, [P, R, P], F32) for n in ("u_r", "p_r", "w_r"))
+        u, v, p, w5 = (four(n, MAIN) for n in ("u", "v", "p", "w5_"))
+        u_rest, p_rest, w5_rest = (new(n, [P, R, P], F32) for n in ("u_rest", "p_rest", "w5_rest"))
 
-        def leave_banks(t):
+        def leave_d_and_y(t):
             if t not in d_ps:
-                d_ps[t] = project(2, t, x_two, 2 + t)
+                d_ps[t] = project(2, t, x_two, D_BANKS[t])
             nc.scalar.copy(d[t][:], d_ps[t][:])
             for c0 in (0, HALF):
-                nc.scalar.activation(yh_gate[t][:, S + c0 : S + c0 + HALF], d[t][:].indirect(entries("n2", c0, HALF)), ACT.Sigmoid)
+                gate = yh_gate[t][:, S + c0 : S + c0 + HALF]
+                nc.scalar.activation(gate, looked_up(d[t], "n2", slice(c0, c0 + HALF)), ACT.Sigmoid)
             nc.scalar.activation(yh_gate[t][:, 0:S], y_ps[t][:], ACT.Copy, scale=-0.5)
 
-        def make_bg(t):
-            acc = project(3, t, x_three, t % 2)
-            nc.scalar.activation(bg[t][:], acc[:], ACT.Copy, scale=half_gain[:, t : t + 1])
+        def make_bh(t):
+            acc = project(3, t, x_three, B_BANKS[t])
+            nc.scalar.activation(bh[t][:], acc[:], ACT.Copy, scale=half_gain[:, t : t + 1])
 
-        def make_yg(t):
-            nc.vector.scalar_tensor_tensor(yg[t][:], yh_gate[t][:, 0:S], -2.0, yh_gate[t][:, S : 2 * S], ALU.mult, ALU.mult)
+        def make_y_gated(t):
+            nc.vector.scalar_tensor_tensor(y_gated[t][:], yh_gate[t][:, 0:S], -2.0, yh_gate[t][:, S : 2 * S], ALU.mult, ALU.mult)
 
         def make_m1(t):
-            nc.vector.tensor_tensor(m1[t][:, 0:S], yh_gate[t][:].indirect(lists["n1"][:]), yg[t][:], ALU.add)
-            nc.scalar.copy(m1c[t][:], m1[t][:, 0:S])
+            nc.vector.tensor_tensor(m1_wide[t][:, 0:S], yh_gate[t][:].indirect(lists["n1"][:]), y_gated[t][:], ALU.add)
+            nc.scalar.copy(m1[t][:], m1_wide[t][:, 0:S])
 
         def fetch(dst, window, name, cols, other, op):
-            nc.vector.tensor_tensor(dst, window[:].indirect(lists[name][:, cols.start // 16 : cols.stop // 16]), other, op)
+            nc.vector.tensor_tensor(dst, looked_up(window, name, cols), other, op)
 
         def make_p(dst, t, cols, diff):
-            nc.vector.scalar_tensor_tensor(dst, bg[t][:, cols], 2.0, diff, ALU.mult, ALU.mult)
+            nc.vector.scalar_tensor_tensor(dst, bh[t][:, cols], 2.0, diff, ALU.mult, ALU.mult)
 
         def turn_sum(acc, first, second):
             nc.tensor.matmul(acc, first, ident[:], start=True, stop=False, is_transpose=True)
@@ -200,97 +211,109 @@ def tile_picked_triogatebflowbmed_none_po_kernel(
 
         blocks = [slice(P * i, P * (i + 1)) for i in range(MAIN // P)]
         z_turned = []
+        z_words = []
 
         def sum_z(t):
             for i, cols in enumerate(blocks):
                 if t == 0:
-                    z_turned.append(bank((2, 3, 6)[i], [P, R, P]))
+                    z_turned.append(bank(Z_SUM_BANKS[i], [P, R, P]))
                 turn_sum(z_turned[i][:, t, :], p[t][:, cols], w5[t][:, cols])
 
-        def turn_z_back(i, words_ps, dst):
-            pairs = new("z_pairs%d" % i, [P, 2, P, 2], BF16)
-            nc.scalar.copy(pairs[:], z_turned[i][:].rearrange("q (u e) p -> q u p e", e=2))
-            words = pairs[:].rearrange("q u p e -> q (u p e)").bitcast(F32)
-            for half in range(2):
-                nc.tensor.transpose(words_ps[:, half, :], words[:, P * half : P * (half + 1)], ident[:])
-            nc.scalar.copy(dst.rearrange("p q t -> p (q t)").bitcast(F32).rearrange("p (q u) -> p q u", u=2), words_ps.rearrange("p u q -> p q u"))
+        def turn_z_back(pair):
+            if pair == 0:
+                two_blocks = bank(Z_WORD_BANKS[0], [P, 2, 2, P])
+                one_block = bank(Z_WORD_BANKS[1], [P, 2, P])
+                z_words.extend([two_blocks[:, 0, :, :], two_blocks[:, 1, :, :], one_block[:]])
+            for i in range(len(blocks)):
+                rounded = new("z_rounded%d_%d" % (pair, i), [P, P, 2], BF16)
+                nc.scalar.copy(rounded[:], z_turned[i][:, 2 * pair : 2 * pair + 2, :].rearrange("q e p -> q p e"))
+                nc.tensor.transpose(z_words[i][:, pair, :], rounded[:].rearrange("q p e -> q (p e)").bitcast(F32), ident[:])
+
+        def leave_z_words(i, dst):
+            as_words = dst.rearrange("p q t -> p (q t)").bitcast(F32).rearrange("p (q r) -> p q r", r=2)
+            nc.scalar.copy(as_words, z_words[i].rearrange("p r q -> p q r"))
 
         def last_layer(name, woven, n, outs):
-            zq = new("zq" + name, [P, n], U32)
-            zs = new("zs" + name, [P, n], U8)
-            nc.vector.quantize_mx(out=zq[:].bitcast(FP8X4), scales=zs[:], in_=woven[:].rearrange("p c t -> p (c t)"))
+            codes = new("z_codes_" + name, [P, n], U32)
+            scales = new("z_scales_" + name, [P, n], U8)
+            nc.vector.quantize_mx(out=codes[:].bitcast(FP8X4), scales=scales[:], in_=woven[:].rearrange("p c t -> p (c t)"))
             for t in range(R):
-                product(outs[t], 4, t, zq[:], zs[:])
-            return zq
+                product(outs[t], 4, t, codes[:], scales[:])
 
-        leave_banks(0)
-        leave_banks(1)
-        make_yg(0)
+        leave_d_and_y(0)
+        leave_d_and_y(1)
+        make_y_gated(0)
         make_m1(0)
-        make_bg(0)
+        make_bh(0)
         for t in range(R):
             if t + 1 < R:
-                make_bg(t + 1)
+                make_bh(t + 1)
             if t + 2 < R:
-                leave_banks(t + 2)
+                leave_d_and_y(t + 2)
             if t + 1 < R:
-                make_yg(t + 1)
-            fetch(v[t][:], m1[t], "n4", main, m1c[t][:, main], ALU.subtract)
-            fetch(u[t][:], m1[t], "n3", main, m1c[t][:, main], ALU.subtract)
+                make_y_gated(t + 1)
+            fetch(v[t][:], m1_wide[t], "n4", main, m1[t][:, main], ALU.subtract)
+            fetch(u[t][:], m1_wide[t], "n3", main, m1[t][:, main], ALU.subtract)
             if t + 1 < R:
                 make_m1(t + 1)
-            fetch(w5[t][:], bg[t], "n5", main, v[t][:], ALU.mult)
+            fetch(w5[t][:], bh[t], "n5", main, v[t][:], ALU.mult)
             make_p(p[t][:], t, main, u[t][:])
             sum_z(t)
+            if t % 2 == 1:
+                turn_z_back(t // 2)
 
-        deal_words(4, "v%d" % (R - 1))
-        deal_scales(4, "u%d" % (R - 1))
-        zb_a = new("zb_a", [P, HALF, R], BF16, tag="zb_a")
-        zb_b = new("zb_b", [P, P, R], BF16, tag="zb_b")
-        zb_r = new("zb_r", [P, P, R], BF16)
-        words_a = bank(7, [P, 2, 2, P])
-        words_b = bank(0, [P, 2, P])
-        turn_z_back(0, words_a[:, 0, :, :], zb_a[:, 0:P, :])
-        turn_z_back(1, words_a[:, 1, :, :], zb_a[:, P:HALF, :])
-        turn_z_back(2, words_b[:], zb_b[:])
-        h_ps = [bank(number, [P, MAIN]) for number in (1, 4, 5, 7)]
+        final = R - 1
+        deal_words(4, "v%d" % final)
+        deal_scales(4, "u%d" % final)
+        z_woven_a = new("z_woven_a", [P, HALF, R], BF16, tag="z_woven_a")
+        z_woven_b = new("z_woven_b", [P, P, R], BF16, tag="z_woven_b")
+        z_woven_rest = new("z_woven_rest", [P, P, R], BF16)
+        leave_z_words(0, z_woven_a[:, 0:P, :])
+        leave_z_words(1, z_woven_a[:, P:HALF, :])
+        leave_z_words(2, z_woven_b[:])
+        h_ps = [bank(number, [P, MAIN]) for number in H_BANKS]
 
-        def leave_h(t):
-            nc.scalar.copy(hw[t][:, main], h_ps[t][:])
-            nc.scalar.copy(hc[t][:, main], h_ps[t][:])
+        def leave_h_main(t):
+            nc.scalar.copy(h_wide[t][:, main], h_ps[t][:])
+            nc.scalar.copy(h[t][:, main], h_ps[t][:])
 
+        z_rest = new("z_rest", [P, R, P], F32)
+        behind = {final - 1: "z_woven_a", final: "z_woven_b"}
         for t in range(R):
-            if t == R - 1:
-                last_layer("a", zb_a, HALF, [h_ps[i][:, 0:HALF] for i in range(R)])
-            v_r = new("v_r%d" % t, [P, P], F32, tag="zb_a" if t == R - 1 else "")
-            fetch(v_r[:], m1c[t], "n4", rest, m1[t][:, rest], ALU.subtract)
-            fetch(u_r[:, t, :], m1c[t], "n3", rest, m1[t][:, rest], ALU.subtract)
-            if t == R - 1:
-                last_layer("b", zb_b, P, [h_ps[i][:, HALF:MAIN] for i in range(R)])
-                z_r = new("z_r", [P, R, P], F32, tag="zb_b")
-                nc.vector.tensor_tensor(z_r[:, 0:t, :], p_r[:, 0:t, :], w_r[:, 0:t, :], ALU.add)
-            fetch(w_r[:, t, :], bg[t], "n5", rest, v_r[:], ALU.mult)
-            make_p(p_r[:, t, :], t, rest, u_r[:, t, :])
-        nc.vector.tensor_tensor(z_r[:, R - 1, :], p_r[:, R - 1, :], w_r[:, R - 1, :], ALU.add)
-        weave(nc.vector.tensor_copy, zb_r[:], z_r[:])
-        leave_h(0)
-        leave_h(1)
-        h_r = [bank(number, [P, 2, P]) for number in (0, 6)]
-        zq_last = last_layer("r", zb_r, P, [h_r[i // 2][:, i % 2, :] for i in range(R)])
+            if t == final - 1:
+                last_layer("a", z_woven_a, HALF, [acc[:, 0:HALF] for acc in h_ps])
+            if t == final:
+                last_layer("b", z_woven_b, P, [acc[:, HALF:MAIN] for acc in h_ps])
+            v_rest = new("v_rest%d" % t, [P, P], F32, tag=behind.get(t, ""))
+            fetch(v_rest[:], m1[t], "n4", rest, m1_wide[t][:, rest], ALU.subtract)
+            fetch(u_rest[:, t, :], m1[t], "n3", rest, m1_wide[t][:, rest], ALU.subtract)
+            if t == final:
+                nc.vector.tensor_tensor(z_rest[:, 0:final, :], p_rest[:, 0:final, :], w5_rest[:, 0:final, :], ALU.add)
+            fetch(w5_rest[:, t, :], bh[t], "n5", rest, v_rest[:], ALU.mult)
+            make_p(p_rest[:, t, :], t, rest, u_rest[:, t, :])
+        nc.vector.tensor_tensor(z_rest[:, final, :], p_rest[:, final, :], w5_rest[:, final, :], ALU.add)
+        weave(nc.vector.tensor_copy, z_woven_rest[:], z_rest[:])
+        leave_h_main(0)
+        leave_h_main(1)
+        h_rest_ps = [bank(number, [P, 2, P]) for number in H_REST_BANKS]
+        h_rest = [h_rest_ps[t // 2][:, t % 2, :] for t in range(R)]
+        last_layer("rest", z_woven_rest, P, h_rest)
+        nc.vector.tensor_copy(h_wide[0][:, rest], h_rest[0])
+        nc.scalar.copy(h_wide[1][:, rest], h_rest[1])
+        for t in range(2, R):
+            leave_h_main(t)
+            nc.scalar.copy(h_wide[t][:, rest], h_rest[t])
         for t in range(R):
-            if t > 1:
-                leave_h(t)
-            leave = nc.vector.tensor_copy if t == 0 else nc.scalar.copy
-            leave(hw[t][:, rest], h_r[t // 2][:, t % 2, :])
-        for t in range(R):
-            nc.scalar.copy(hc[t][:, rest], h_r[t // 2][:, t % 2, :])
+            nc.scalar.copy(h[t][:, rest], h_rest[t])
 
-        oq = new("oq", [P, S], U32)
-        osc = new("osc", [P, S], U8)
+        out_codes = new("out_codes", [P, S], U32)
+        out_scales = new("out_scales", [P, S], U8)
         out_rows = out_0.rearrange("(p t) s -> p t s", t=R)
         out_words = out_1[0].rearrange("p n t -> p (n t)").bitcast(I32)
-        da, db, lo, med = (rows(n, MAIN) for n in ("da", "db", "lo", "med"))
-        da_r, db_r, lo_r, med_r, res_r = (new(n, [P, R, P], F32) for n in ("da_r", "db_r", "lo_r", "med_r", "res_r"))
+        da, db, upper, med = (four(n, MAIN) for n in ("da", "db", "upper", "med"))
+        da_rest, db_rest, upper_rest, med_rest, res_rest = (
+            new(n, [P, R, P], F32) for n in ("da_rest", "db_rest", "upper_rest", "med_rest", "res_rest")
+        )
         res = new("res", [P, R, MAIN], F32)
 
         def clip_above(dst, first, second):
@@ -300,56 +323,59 @@ def tile_picked_triogatebflowbmed_none_po_kernel(
             nc.vector.scalar_tensor_tensor(dst, first, 0.0, clipped, ALU.min, ALU.max)
 
         def add_h(t):
-            turned = bank(2 + t % 2, [P, MAIN])
+            turned = bank(OUT_SUM_BANKS[t % 2], [P, MAIN])
             for cols in blocks:
-                turn_sum(turned[:, cols], hc[t][:, cols], med[t][:, cols])
+                turn_sum(turned[:, cols], h[t][:, cols], med[t][:, cols])
             staged = new("staged%d" % t, [P, MAIN], F32)
             nc.scalar.copy(staged[:], turned[:])
-            back = bank((1, 4, 5, 7)[t], [P, MAIN])
+            back = bank(H_BANKS[t], [P, MAIN])
             for cols in blocks:
                 nc.tensor.transpose(back[:, cols], staged[:, cols], ident[:])
             nc.scalar.copy(res[:, t, :], back[:])
             nc.sync.dma_start(out_rows[:, t, main], res[:, t, :])
 
-        def planes(woven, cols):
-            nc.vector.quantize_mx(out=oq[:, cols].bitcast(FP8X4), scales=osc[:, cols], in_=woven[:].rearrange("p c t -> p (c t)"))
+        def quantise_out(woven, cols):
+            nc.vector.quantize_mx(
+                out=out_codes[:, cols].bitcast(FP8X4), scales=out_scales[:, cols], in_=woven[:].rearrange("p c t -> p (c t)")
+            )
 
-        for t in range(R + 1):
-            if t < R:
-                fetch(da[t][:], hw[t], "n6", main, hc[t][:, main], ALU.subtract)
-            else:
-                fetch(da_r[:, 0, :], hc[0], "n6", rest, hw[0][:, rest], ALU.subtract)
+        for t in range(R):
+            fetch(da[t][:], h_wide[t], "n6", main, h[t][:, main], ALU.subtract)
             if t > 0:
-                clip_above(lo[t - 1][:], da[t - 1][:], db[t - 1][:])
-            if t < R:
-                fetch(db[t][:], hw[t], "n7", main, hc[t][:, main], ALU.subtract)
-            else:
-                fetch(db_r[:, 0, :], hc[0], "n7", rest, hw[0][:, rest], ALU.subtract)
+                clip_above(upper[t - 1][:], da[t - 1][:], db[t - 1][:])
+            fetch(db[t][:], h_wide[t], "n7", main, h[t][:, main], ALU.subtract)
             if t > 0:
-                clip_below(med[t - 1][:], da[t - 1][:], lo[t - 1][:])
+                clip_below(med[t - 1][:], da[t - 1][:], upper[t - 1][:])
                 add_h(t - 1)
-        resb_a = new("resb_a", [P, HALF, R], BF16)
-        resb_b = new("resb_b", [P, P, R], BF16)
-        resb_r = new("resb_r", [P, P, R], BF16)
-        weave(nc.scalar.copy, resb_a[:], res[:, :, 0:HALF])
-        weave(nc.scalar.copy, resb_b[:], res[:, :, HALF:MAIN])
+        clip_above(upper[final][:], da[final][:], db[final][:])
+        fetch(da_rest[:, 0, :], h[0], "n6", rest, h_wide[0][:, rest], ALU.subtract)
+        clip_below(med[final][:], da[final][:], upper[final][:])
+        fetch(db_rest[:, 0, :], h[0], "n7", rest, h_wide[0][:, rest], ALU.subtract)
+        nc.vector.tensor_tensor(res[:, final, :], med[final][:], h[final][:, main], ALU.add)
+        nc.sync.dma_start(out_rows[:, final, main], res[:, final, :])
+        res_woven_a = new("res_woven_a", [P, HALF, R], BF16)
+        res_woven_b = new("res_woven_b", [P, P, R], BF16)
+        res_woven_rest = new("res_woven_rest", [P, P, R], BF16)
+        weave(nc.scalar.copy, res_woven_a[:], res[:, :, 0:HALF])
+        weave(nc.scalar.copy, res_woven_b[:], res[:, :, HALF:MAIN])
+
         for t in range(1, R):
-            fetch(da_r[:, t, :], hc[t], "n6", rest, hw[t][:, rest], ALU.subtract)
-            fetch(db_r[:, t, :], hc[t], "n7", rest, hw[t][:, rest], ALU.subtract)
-        pairs_of_t = (slice(0, 2), slice(2, 4))
-        for ts in pairs_of_t:
-            clip_above(lo_r[:, ts, :], da_r[:, ts, :], db_r[:, ts, :])
-        for ts in pairs_of_t:
-            clip_below(med_r[:, ts, :], da_r[:, ts, :], lo_r[:, ts, :])
-        for ts, acc in zip(pairs_of_t, h_r):
-            nc.vector.tensor_tensor(res_r[:, ts, :], med_r[:, ts, :], acc[:], ALU.add)
-        nc.sync.dma_start(out_rows[:, :, rest], res_r[:])
-        planes(resb_a, slice(0, HALF))
-        weave(nc.vector.tensor_copy, resb_r[:], res_r[:])
-        planes(resb_b, slice(HALF, MAIN))
-        nc.sync.dma_start(out_words[:, main], oq[:, main].bitcast(I32))
-        planes(resb_r, rest)
-        nc.sync.dma_start(out_words[:, rest], oq[:, rest].bitcast(I32))
+            fetch(da_rest[:, t, :], h[t], "n6", rest, h_wide[t][:, rest], ALU.subtract)
+            fetch(db_rest[:, t, :], h[t], "n7", rest, h_wide[t][:, rest], ALU.subtract)
+        tile_pairs = (slice(0, 2), slice(2, 4))
+        for ts in tile_pairs:
+            clip_above(upper_rest[:, ts, :], da_rest[:, ts, :], db_rest[:, ts, :])
+        for ts in tile_pairs:
+            clip_below(med_rest[:, ts, :], da_rest[:, ts, :], upper_rest[:, ts, :])
+        for ts, acc in zip(tile_pairs, h_rest_ps):
+            nc.vector.tensor_tensor(res_rest[:, ts, :], med_rest[:, ts, :], acc[:], ALU.add)
+        nc.sync.dma_start(out_rows[:, :, rest], res_rest[:])
+        quantise_out(res_woven_a, slice(0, HALF))
+        weave(nc.vector.tensor_copy, res_woven_rest[:], res_rest[:])
+        quantise_out(res_woven_b, slice(HALF, MAIN))
+        nc.sync.dma_start(out_words[:, main], out_codes[:, main].bitcast(I32))
+        quantise_out(res_woven_rest, rest)
+        nc.sync.dma_start(out_words[:, rest], out_codes[:, rest].bitcast(I32))
         for q in range(4):
             queue = nc.scalar if q % 2 else nc.sync
-            queue.dma_start(out_2[0, 4 * q : 4 * q + 4, :].bitcast(I32), osc[32 * q : 32 * q + 4, :].bitcast(I32))
+            queue.dma_start(out_2[0, 4 * q : 4 * q + 4, :].bitcast(I32), out_scales[32 * q : 32 * q + 4, :].bitcast(I32))

from contextlib import ExitStack

import concourse.mybir as mybir
from concourse.masks import make_identity

F32 = mybir.dt.float32
BF16 = mybir.dt.bfloat16
I32 = mybir.dt.int32
U32 = mybir.dt.uint32
U16 = mybir.dt.uint16
U8 = mybir.dt.uint8
FP8X4 = mybir.dt.float8_e4m3fn_x4
FP4X4 = mybir.dt.float4_e2m1fn_x4
ALU = mybir.AluOpType
ACT = mybir.ActivationFunctionType

P = 128
R = 4
T = 2048
S = 512
HALF = S // 2
MAIN = 3 * P
WIDE = 2 * MAIN
PER_COLUMN = 16
FLOPS = 4 * 2 * 512 * 512 * 512

D_BANKS = (0, 1, 4, 5)
Y_BANKS = (4, 5, 6, 7)
B_BANKS = (0, 1, 0, 1)
Z_SUM_BANKS = (2, 3, 6)
Z_WORD_BANKS = (7, 0)
H_BANKS = (1, 4, 5, 7)
H_REST_BANKS = (0, 6)
OUT_SUM_BANKS = (2, 3)


def tile_picked_triogatebflowbmed_none_po_kernel(
    tc, x_words, x_scales, w1_words, w1_scales, w2_words, w2_scales, w3_words, w3_scales, gn,
    w4_words, w4_scales, offs, two, three, n1, n2, n3, n4, n5, n6, n7, out_0, out_1, out_2,
):
    nc = tc.nc
    with ExitStack() as ctx:
        sb = ctx.enter_context(tc.tile_pool(name="sb", bufs=1))
        ps = ctx.enter_context(tc.psum_pool(name="ps", bufs=1))

        def new(name, shape, dtype, tag=""):
            return sb.tile(shape, dtype, name=name, tag=tag, align_bytes=64)

        def four(name, width):
            return [new("%s%d" % (name, t), [P, width], F32, tag="%s%d" % (name, t)) for t in range(R)]

        def bank(number, shape):
            return ps.tile(shape, F32, name="bank%d" % number)

        lists = {}

        def load_list(name, src):
            lists[name] = new("list_" + name, [P, S // PER_COLUMN], U16)
            nc.sync.dma_start(lists[name][:], src)

        def looked_up(window, name, cols):
            return window[:].indirect(lists[name][:, cols.start // PER_COLUMN : cols.stop // PER_COLUMN])

        def load_scale_rows(dst, src):
            for q in range(4):
                nc.sync.dma_start(dst[32 * q : 32 * q + 4, :].bitcast(I32), src[0, 4 * q : 4 * q + 4, :].bitcast(I32))

        x_scale_rows = new("x_scale_rows", [P, T], U8)
        nc.vector.memset(x_scale_rows[:].bitcast(I32), 0)
        raw_scales = {}
        for w in (2, 1, 3, 4):
            raw_scales[w] = new("raw_scales%d" % w, [P, S], U8, tag="raw_scales%d" % w)
            nc.vector.memset(raw_scales[w][:].bitcast(I32), 0)

        warm_in = new("warm_in", [P, 1], F32)
        warm_out = new("warm_out", [P, 1], F32)
        nc.vector.memset(warm_in[:], 0.0)
        nc.scalar.activation(warm_out[:], warm_in[:], ACT.Sigmoid)

        w_words = {1: w1_words, 2: w2_words, 3: w3_words, 4: w4_words}
        w_scales = {1: w1_scales, 2: w2_scales, 3: w3_scales, 4: w4_scales}
        raw_words = {}

        def load_words(w):
            raw_words[w] = new("raw_words%d" % w, [P, 2 * S], U8)
            nc.sync.dma_start(raw_words[w][:].bitcast(I32), w_words[w][0].bitcast(I32))

        load_words(2)
        load_list("two", two)
        load_list("offs", offs)
        load_scale_rows(x_scale_rows, x_scales)
        x_table = new("x_table", [P, T], I32)
        nc.sync.dma_start(x_table[:], x_words[0].rearrange("p n t -> p (n t)").bitcast(I32))
        load_scale_rows(raw_scales[2], w_scales[2])
        load_words(1)
        load_list("n2", n2)
        load_scale_rows(raw_scales[1], w_scales[1])
        load_list("three", three)
        load_words(3)
        load_list("n1", n1)
        gain = new("gain", [P, R], F32)
        nc.sync.dma_start(gain[:], gn.rearrange("(p t) o -> p (t o)", t=R))
        load_scale_rows(raw_scales[3], w_scales[3])
        load_list("n4", n4)
        load_list("n3", n3)
        load_list("n5", n5)
        load_words(4)
        load_scale_rows(raw_scales[4], w_scales[4])
        load_list("n6", n6)
        load_list("n7", n7)

        dealt_words = {}
        dealt_scales = {}

        def deal_words(w, tag=""):
            dealt_words[w] = new("dealt_words%d" % w, [P, 2 * S], U8, tag=tag)
            nc.vector.tensor_copy(
                dealt_words[w][:].rearrange("p (t m b) -> p t m b", t=R, b=2),
                raw_words[w][:].rearrange("p (m t b) -> p t m b", t=R, b=2),
            )

        def deal_scales(w, tag=""):
            dealt_scales[w] = new("dealt_scales%d" % w, [P, S], U8, tag=tag)
            nc.vector.tensor_copy(
                dealt_scales[w][:].rearrange("p (t m) -> p t m", t=R),
                raw_scales[w][:].rearrange("p (m t) -> p t m", t=R),
            )

        def product(acc, w, t, codes, scales):
            nc.tensor.matmul_mx(
                out=acc,
                lhsT=dealt_words[w][:, 2 * P * t : 2 * P * (t + 1)].bitcast(FP4X4),
                lhsT_scale=dealt_scales[w][:, P * t : P * (t + 1)],
                rhs=codes.bitcast(FP8X4),
                rhs_scale=scales,
                start=True,
                stop=True,
            )

        def pick(name, tag=""):
            codes = new("codes_" + name, [P, S], U32, tag=tag)
            scales = new("scales_" + name, [P, S], U8)
            nc.vector.tensor_copy(scales[:], x_scale_rows[:].indirect(lists[name][:]))
            nc.vector.tensor_copy(codes[:], x_table[:].bitcast(U32).indirect(lists[name][:]))
            return codes, scales

        def project(w, t, picked, number):
            acc = bank(number, [P, S])
            product(acc[:], w, t, picked[0][:], picked[1][:])
            return acc

        ident = new("ident", [P, P], F32)
        make_identity(nc, ident[:])
        half_gain = new("half_gain", [P, R], F32)
        nc.scalar.activation(half_gain[:], gain[:], ACT.Copy, scale=0.5)

        m1_wide, h_wide = four("m1_wide", WIDE), four("h_wide", WIDE)
        for window in m1_wide + h_wide:
            nc.gpsimd.memset(window[:, S:WIDE], 0.0)

        deal_words(2)
        x_two = pick("two")
        deal_scales(2)
        d_ps = {t: project(2, t, x_two, D_BANKS[t]) for t in range(2)}
        x_offs = pick("offs", "raw_scales2")
        deal_words(1)
        deal_scales(1)
        y_ps = [project(1, t, x_offs, Y_BANKS[t]) for t in range(R)]
        x_three = pick("three", "raw_scales1")
        deal_words(3)
        deal_scales(3)

        d, y_gated, m1, bh, h = (four(n, S) for n in ("d", "y_gated", "m1", "bh", "h"))
        yh_gate = four("yh_gate", 2 * S)
        main, rest = slice(0, MAIN), slice(MAIN, S)
        u, v, p, w5 = (four(n, MAIN) for n in ("u", "v", "p", "w5_"))
        u_rest, p_rest, w5_rest = (new(n, [P, R, P], F32) for n in ("u_rest", "p_rest", "w5_rest"))

        def leave_d_and_y(t):
            if t not in d_ps:
                d_ps[t] = project(2, t, x_two, D_BANKS[t])
            nc.scalar.copy(d[t][:], d_ps[t][:])
            for c0 in (0, HALF):
                gate = yh_gate[t][:, S + c0 : S + c0 + HALF]
                nc.scalar.activation(gate, looked_up(d[t], "n2", slice(c0, c0 + HALF)), ACT.Sigmoid)
            nc.scalar.activation(yh_gate[t][:, 0:S], y_ps[t][:], ACT.Copy, scale=-0.5)

        def make_bh(t):
            acc = project(3, t, x_three, B_BANKS[t])
            nc.scalar.activation(bh[t][:], acc[:], ACT.Copy, scale=half_gain[:, t : t + 1])

        def make_y_gated(t):
            nc.vector.scalar_tensor_tensor(y_gated[t][:], yh_gate[t][:, 0:S], -2.0, yh_gate[t][:, S : 2 * S], ALU.mult, ALU.mult)

        def make_m1(t):
            nc.vector.tensor_tensor(m1_wide[t][:, 0:S], yh_gate[t][:].indirect(lists["n1"][:]), y_gated[t][:], ALU.add)
            nc.scalar.copy(m1[t][:], m1_wide[t][:, 0:S])

        def fetch(dst, window, name, cols, other, op):
            nc.vector.tensor_tensor(dst, looked_up(window, name, cols), other, op)

        def make_p(dst, t, cols, diff):
            nc.vector.scalar_tensor_tensor(dst, bh[t][:, cols], 2.0, diff, ALU.mult, ALU.mult)

        def turn_sum(acc, first, second):
            nc.tensor.matmul(acc, first, ident[:], start=True, stop=False, is_transpose=True)
            nc.tensor.matmul(acc, second, ident[:], start=False, stop=True, is_transpose=True)

        def weave(engine_copy, dst, src):
            engine_copy(dst.rearrange("p (c i) t -> p c t i", i=4), src.rearrange("p t (c i) -> p c t i", i=4))

        blocks = [slice(P * i, P * (i + 1)) for i in range(MAIN // P)]
        z_turned = []
        z_words = []

        def sum_z(t):
            for i, cols in enumerate(blocks):
                if t == 0:
                    z_turned.append(bank(Z_SUM_BANKS[i], [P, R, P]))
                turn_sum(z_turned[i][:, t, :], p[t][:, cols], w5[t][:, cols])

        def turn_z_back(pair):
            if pair == 0:
                two_blocks = bank(Z_WORD_BANKS[0], [P, 2, 2, P])
                one_block = bank(Z_WORD_BANKS[1], [P, 2, P])
                z_words.extend([two_blocks[:, 0, :, :], two_blocks[:, 1, :, :], one_block[:]])
            for i in range(len(blocks)):
                rounded = new("z_rounded%d_%d" % (pair, i), [P, P, 2], BF16)
                nc.scalar.copy(rounded[:], z_turned[i][:, 2 * pair : 2 * pair + 2, :].rearrange("q e p -> q p e"))
                nc.tensor.transpose(z_words[i][:, pair, :], rounded[:].rearrange("q p e -> q (p e)").bitcast(F32), ident[:])

        def leave_z_words(i, dst):
            as_words = dst.rearrange("p q t -> p (q t)").bitcast(F32).rearrange("p (q r) -> p q r", r=2)
            nc.scalar.copy(as_words, z_words[i].rearrange("p r q -> p q r"))

        def last_layer(name, woven, n, outs):
            codes = new("z_codes_" + name, [P, n], U32)
            scales = new("z_scales_" + name, [P, n], U8)
            nc.vector.quantize_mx(out=codes[:].bitcast(FP8X4), scales=scales[:], in_=woven[:].rearrange("p c t -> p (c t)"))
            for t in range(R):
                product(outs[t], 4, t, codes[:], scales[:])

        leave_d_and_y(0)
        leave_d_and_y(1)
        make_y_gated(0)
        make_m1(0)
        make_bh(0)
        for t in range(R):
            if t + 1 < R:
                make_bh(t + 1)
            if t + 2 < R:
                leave_d_and_y(t + 2)
            if t + 1 < R:
                make_y_gated(t + 1)
            fetch(v[t][:], m1_wide[t], "n4", main, m1[t][:, main], ALU.subtract)
            fetch(u[t][:], m1_wide[t], "n3", main, m1[t][:, main], ALU.subtract)
            if t + 1 < R:
                make_m1(t + 1)
            fetch(w5[t][:], bh[t], "n5", main, v[t][:], ALU.mult)
            make_p(p[t][:], t, main, u[t][:])
            sum_z(t)
            if t % 2 == 1:
                turn_z_back(t // 2)

        final = R - 1
        deal_words(4, "v%d" % final)
        deal_scales(4, "u%d" % final)
        z_woven_a = new("z_woven_a", [P, HALF, R], BF16, tag="z_woven_a")
        z_woven_b = new("z_woven_b", [P, P, R], BF16, tag="z_woven_b")
        z_woven_rest = new("z_woven_rest", [P, P, R], BF16)
        leave_z_words(0, z_woven_a[:, 0:P, :])
        leave_z_words(1, z_woven_a[:, P:HALF, :])
        leave_z_words(2, z_woven_b[:])
        h_ps = [bank(number, [P, MAIN]) for number in H_BANKS]

        def leave_h_main(t):
            nc.scalar.copy(h_wide[t][:, main], h_ps[t][:])
            nc.scalar.copy(h[t][:, main], h_ps[t][:])

        z_rest = new("z_rest", [P, R, P], F32)
        behind = {final - 1: "z_woven_a", final: "z_woven_b"}
        for t in range(R):
            if t == final - 1:
                last_layer("a", z_woven_a, HALF, [acc[:, 0:HALF] for acc in h_ps])
            if t == final:
                last_layer("b", z_woven_b, P, [acc[:, HALF:MAIN] for acc in h_ps])
            v_rest = new("v_rest%d" % t, [P, P], F32, tag=behind.get(t, ""))
            fetch(v_rest[:], m1[t], "n4", rest, m1_wide[t][:, rest], ALU.subtract)
            fetch(u_rest[:, t, :], m1[t], "n3", rest, m1_wide[t][:, rest], ALU.subtract)
            if t == final:
                nc.vector.tensor_tensor(z_rest[:, 0:final, :], p_rest[:, 0:final, :], w5_rest[:, 0:final, :], ALU.add)
            fetch(w5_rest[:, t, :], bh[t], "n5", rest, v_rest[:], ALU.mult)
            make_p(p_rest[:, t, :], t, rest, u_rest[:, t, :])
        nc.vector.tensor_tensor(z_rest[:, final, :], p_rest[:, final, :], w5_rest[:, final, :], ALU.add)
        weave(nc.vector.tensor_copy, z_woven_rest[:], z_rest[:])
        leave_h_main(0)
        leave_h_main(1)
        h_rest_ps = [bank(number, [P, 2, P]) for number in H_REST_BANKS]
        h_rest = [h_rest_ps[t // 2][:, t % 2, :] for t in range(R)]
        last_layer("rest", z_woven_rest, P, h_rest)
        nc.vector.tensor_copy(h_wide[0][:, rest], h_rest[0])
        nc.scalar.copy(h_wide[1][:, rest], h_rest[1])
        for t in range(2, R):
            leave_h_main(t)
            nc.scalar.copy(h_wide[t][:, rest], h_rest[t])
        for t in range(R):
            nc.scalar.copy(h[t][:, rest], h_rest[t])

        out_codes = new("out_codes", [P, S], U32)
        out_scales = new("out_scales", [P, S], U8)
        out_rows = out_0.rearrange("(p t) s -> p t s", t=R)
        out_words = out_1[0].rearrange("p n t -> p (n t)").bitcast(I32)
        da, db, upper, med = (four(n, MAIN) for n in ("da", "db", "upper", "med"))
        da_rest, db_rest, upper_rest, med_rest, res_rest = (
            new(n, [P, R, P], F32) for n in ("da_rest", "db_rest", "upper_rest", "med_rest", "res_rest")
        )
        res = new("res", [P, R, MAIN], F32)

        def clip_above(dst, first, second):
            nc.vector.scalar_tensor_tensor(dst, first, 0.0, second, ALU.max, ALU.min)

        def clip_below(dst, first, clipped):
            nc.vector.scalar_tensor_tensor(dst, first, 0.0, clipped, ALU.min, ALU.max)

        def add_h(t):
            turned = bank(OUT_SUM_BANKS[t % 2], [P, MAIN])
            for cols in blocks:
                turn_sum(turned[:, cols], h[t][:, cols], med[t][:, cols])
            staged = new("staged%d" % t, [P, MAIN], F32)
            nc.scalar.copy(staged[:], turned[:])
            back = bank(H_BANKS[t], [P, MAIN])
            for cols in blocks:
                nc.tensor.transpose(back[:, cols], staged[:, cols], ident[:])
            nc.scalar.copy(res[:, t, :], back[:])
            nc.sync.dma_start(out_rows[:, t, main], res[:, t, :])

        def quantise_out(woven, cols):
            nc.vector.quantize_mx(
                out=out_codes[:, cols].bitcast(FP8X4), scales=out_scales[:, cols], in_=woven[:].rearrange("p c t -> p (c t)")
            )

        for t in range(R):
            fetch(da[t][:], h_wide[t], "n6", main, h[t][:, main], ALU.subtract)
            if t > 0:
                clip_above(upper[t - 1][:], da[t - 1][:], db[t - 1][:])
            fetch(db[t][:], h_wide[t], "n7", main, h[t][:, main], ALU.subtract)
            if t > 0:
                clip_below(med[t - 1][:], da[t - 1][:], upper[t - 1][:])
                add_h(t - 1)
        clip_above(upper[final][:], da[final][:], db[final][:])
        fetch(da_rest[:, 0, :], h[0], "n6", rest, h_wide[0][:, rest], ALU.subtract)
        clip_below(med[final][:], da[final][:], upper[final][:])
        fetch(db_rest[:, 0, :], h[0], "n7", rest, h_wide[0][:, rest], ALU.subtract)
        nc.vector.tensor_tensor(res[:, final, :], med[final][:], h[final][:, main], ALU.add)
        nc.sync.dma_start(out_rows[:, final, main], res[:, final, :])
        res_woven_a = new("res_woven_a", [P, HALF, R], BF16)
        res_woven_b = new("res_woven_b", [P, P, R], BF16)
        res_woven_rest = new("res_woven_rest", [P, P, R], BF16)
        weave(nc.scalar.copy, res_woven_a[:], res[:, :, 0:HALF])
        weave(nc.scalar.copy, res_woven_b[:], res[:, :, HALF:MAIN])

        for t in range(1, R):
            fetch(da_rest[:, t, :], h[t], "n6", rest, h_wide[t][:, rest], ALU.subtract)
            fetch(db_rest[:, t, :], h[t], "n7", rest, h_wide[t][:, rest], ALU.subtract)
        tile_pairs = (slice(0, 2), slice(2, 4))
        for ts in tile_pairs:
            clip_above(upper_rest[:, ts, :], da_rest[:, ts, :], db_rest[:, ts, :])
        for ts in tile_pairs:
            clip_below(med_rest[:, ts, :], da_rest[:, ts, :], upper_rest[:, ts, :])
        for ts, acc in zip(tile_pairs, h_rest_ps):
            nc.vector.tensor_tensor(res_rest[:, ts, :], med_rest[:, ts, :], acc[:], ALU.add)
        nc.sync.dma_start(out_rows[:, :, rest], res_rest[:])
        quantise_out(res_woven_a, slice(0, HALF))
        weave(nc.vector.tensor_copy, res_woven_rest[:], res_rest[:])
        quantise_out(res_woven_b, slice(HALF, MAIN))
        nc.sync.dma_start(out_words[:, main], out_codes[:, main].bitcast(I32))
        quantise_out(res_woven_rest, rest)
        nc.sync.dma_start(out_words[:, rest], out_codes[:, rest].bitcast(I32))
        for q in range(4):
            queue = nc.scalar if q % 2 else nc.sync
            queue.dma_start(out_2[0, 4 * q : 4 * q + 4, :].bitcast(I32), out_scales[32 * q : 32 * q + 4, :].bitcast(I32))
